import numpy as np, ml_dtypes
CORES = [1,5,17,21,33,37,49,53]
N = 8
import mx_ref
BF = ml_dtypes.bfloat16
def cols(t, e):
    v = np.concatenate([t.reshape(128, -1, 4), np.zeros((128, 1, 4), BF)], axis=1)
    return np.ascontiguousarray(v[:, e]).reshape(128, -1)
def cut(t, i, w=512):
    return t[:, w * i:w * i + w]
def f(rng, *shape):
    return mx_ref.flush((rng.standard_normal(shape, dtype=np.float32) * np.exp2(rng.integers(-2, 3, shape[:-1] + (1,)))).astype(BF))
def wide(rng, *shape, cols=0):
    v = rng.standard_normal(shape, dtype=np.float32) * np.exp2(rng.integers(-12, 13, shape)).astype(np.float32)
    if cols: v *= np.repeat(np.exp2(rng.integers(-cols, cols + 1, shape[:-2] + (1, shape[-1] // 4))) * (rng.random(shape[:-2] + (1, shape[-1] // 4)) > 0.0625), 4, axis=-1).astype(np.float32)
    return mx_ref.flush(v.astype(BF))
P, K, R, O = 256, 48, 6, 2
PART = [1, 2, 4, 1, 2, 4]
def scores(c, qt):
    k = mx_ref.quantize(np.concatenate([qt[r][:, :4 * R] for r in range(N)], axis=1))
    s = [mx_ref.matmul(mx_ref.quantize(cut(c[q], i)), k) for q in range(N) for i in range(P // 128)]
    return np.concatenate(s).reshape(N * P, N, R)
def play(s):
    held, use, out = np.arange(N * P).reshape(N, P), np.zeros((N, P), np.float32), []
    for t in range(R):
        left = []
        for r in range(N):
            v = s[held[r], r, t]
            use[r] = use[r] + v * v
            left.append(np.argsort(use[r], kind="stable")[:K])
        new = held.copy()
        for r in range(N):
            p = r ^ PART[t]
            new[r, left[r]] = held[p, left[p]]
            use[r, left[r]] = 0
        held = new
        out.append(held)
    return np.stack(out)
def fit(s):
    a = np.abs(s)
    return bool(np.isfinite(a).all() and ((a == 0) | (a >= 2.0 ** -60) & (a <= 2.0 ** 60)).all())
def times(t, v):
    return mx_ref.flush((t.astype(np.float32) * np.asarray(v, np.float32)).astype(BF))
def plain(rng):
    q = np.array(f(rng, N, 128, 512))
    q[:, :, 4 * R:] = 0
    return {"c": f(rng, N, 128, 4 * P), "qt": q, "w": f(rng, N, 128, 512 * O)}
def first(make, good=None):
    for i in range(50):
        d = make()
        s = scores(d["c"], d["qt"])
        if fit(s) and (good is None or good(s)): return d
    raise RuntimeError("no draw of 50 is fit")
def athome(s):
    h, a = play(s), np.ones((N, R + 1, P), bool)
    for r in range(N):
        for t in range(R): a[r, t + 1] = np.isin(np.arange(P * r, P * r + P), h[t, r])
    return a
def setup_inputs(rng):
    return first(lambda: plain(rng))
def setup_inputs_sides(rng):
    top = np.arange(128) < 64
    def make():
        d = plain(rng)
        half = np.stack([rng.permutation(P) < P // 2 for r in range(N)])
        d["c"] = times(d["c"], np.repeat(half[:, None, :] == top[None, :, None], 4, axis=2))
        for t in range(R):
            g = np.where(top == (PART[t] == 1), 1.0, 2.0 ** -6) * 4.0 ** t
            d["qt"][:, :, 4 * t:4 * t + 4] = times(d["qt"][:, :, 4 * t:4 * t + 4], g[None, :, None])
        return d
    def good(s):
        a = athome(s)
        return bool((~a[:, :-1] & a[:, 1:]).any(axis=(1, 2)).all())
    return first(make, good)
def setup_inputs_ties(rng):
    def make():
        d = plain(rng)
        d["c"] = np.stack([times(cols(d["c"][r], rng.integers(0, 6, P)), np.repeat(1 - 2 * rng.integers(0, 2, P), 4)) for r in range(N)])
        return d
    def good(s):
        for r in range(N):
            v = s[P * r:P * r + P, r, 0]
            u = np.sort(v * v)
            if u[K - 1] != u[K]: return False
        return True
    return first(make, good)
def setup_inputs_shrink(rng):
    low = np.arange(N) >= N - N // 4
    def make():
        d = plain(rng)
        size = np.exp2(np.where(low, -30.0, 23.0)[:, None] + 2 * rng.random((N, P))) * (1 - 2 * rng.integers(0, 2, (N, P)))
        d["c"] = ((1 + rng.random((N, 128, 4 * P))) * np.repeat(size, 4, axis=1)[:, None, :]).astype(np.float32).astype(BF)
        on = ~low[:, None] | np.stack([rng.permutation(128) < 2 for r in range(N)])
        for t in range(R):
            g = np.exp2(np.where(low, 8.0 * (R - 1 - t) - 30.0, 21.0 - 8.0 * t))
            d["qt"][:, :, 4 * t:4 * t + 4] = ((1 + rng.random((N, 128, 4))) * (g[:, None] * on)[:, :, None]).astype(np.float32).astype(BF)
        return d
    def good(s):
        h, a, b = play(s), np.zeros(N, bool), np.zeros(N, bool)
        for r in range(N):
            at, use, since = np.arange(P * r, P * r + P), np.zeros(P, np.float32), np.zeros(P, int)
            if low[r] and np.abs(s[at, r, R - 1]).max() > 2.0 ** -50 or not low[r] and np.abs(s[at, r, 0]).min() < 2.0 ** 50: return False
            for t in range(R):
                v = s[at, r]
                use = use + v[:, t] * v[:, t]
                sums = np.concatenate([np.zeros((P, 1), np.float32), np.cumsum(v * v, axis=1)], axis=1)
                diff = sums[:, t + 1] - sums[np.arange(P), since]
                a[r] |= (np.argsort(use, kind="stable")[:K] != np.argsort(diff, kind="stable")[:K]).any()
                b[r] |= np.sort(use)[K - 1] > 1e30
                moved = h[t, r] != at
                at = h[t, r]
                use[moved] = 0
                since[moved] = t + 1
        return bool(2 * a.sum() > N and 2 * b.sum() > N)
    return first(make, good)
def setup_inputs_turn(rng):
    on = (np.arange(128) // (128 // N))[None, :] == np.arange(N)[:, None]
    def make():
        d = plain(rng)
        d["c"] = times(d["c"], np.where(on, 2.0 ** -8, 1.0)[:, :, None])
        d["qt"] = times(d["qt"], on[:, :, None])
        return d
    return first(make, lambda s: bool((~athome(s)).any(axis=1).all()))
def setup_inputs_spread(rng):
    return first(lambda: {**plain(rng), "c": wide(rng, N, 128, 4 * P, cols=6)})
def check_inputs(d):
    b = []
    for k in ("c", "qt", "w"):
        v = np.abs(d[k].astype(np.float32))
        if not (np.isfinite(v).all() and ((v == 0) | (v >= 2.0 ** -30) & (v <= 2.0 ** 30)).all()): b.append("a value of " + k)
    if (d["qt"][:, :, 4 * R:].astype(np.float32) != 0).any(): b.append("qt has numbers behind its first R columns")
    if not b and not fit(scores(d["c"], d["qt"])): b.append("a score")
    return b
def reference(c, qt, w):
    held = play(scores(c, qt))
    every = np.concatenate([c[q] for q in range(N)], axis=1)
    y = np.zeros((N, 128, R * O * P), np.float32)
    for r in range(N):
        u, at = np.unique(held[:, r].reshape(-1), return_inverse=True)
        at = at.reshape(R, P)
        q = mx_ref.quantize(cols(every, np.concatenate([u, np.full(-len(u) % 4, -1)])))
        for o in range(O):
            z = mx_ref.matmul(mx_ref.quantize(cut(w[r], o)), q)
            for t in range(R):
                i = (t * O + o) * P
                y[r, :, i:i + P] = z[:, at[t]]
    return {"y": y}

@@ -1,0 +1,318 @@
+from concourse.mybir import dt, AluOpType, AxisListType, ActivationFunctionType
+
+N, P, K, R, O = 8, 256, 48, 6, 2
+PART = [1, 2, 4, 1, 2, 4]
+W = [P + K * t for t in range(R)]
+PRED = 1.0 - 2.0 ** -24
+TINY = 2.0 ** -122
+RADIX = 512
+
+SCRATCH = {
+    "cb": ("sbuf", [128, 4 * P], "bfloat16"), "qb": ("sbuf", [128, 512], "bfloat16"), "wb": ("sbuf", [128, 512 * O], "bfloat16"),
+    "qc": ("sbuf", [128, 128], "float8_e4m3fn_x4"), "qs": ("sbuf", [128, 128], "uint8"),
+    "rc": ("sbuf", [128, 128 * R], "float8_e4m3fn_x4"), "rs": ("sbuf", [128, 128 * R], "uint8"),
+    "wc": ("sbuf", [128, 128 * O], "float8_e4m3fn_x4"), "ws": ("sbuf", [128, 128 * O], "uint8"),
+    "qo": ("sbuf", [128, 8 * R], "uint16"),
+    "VZ": ("sbuf", [128, 2 * P], "float32"), "U": ("sbuf", [128, P], "float32"), "F": ("sbuf", [128, P], "float32"),
+    "Y": ("sbuf", [128, O * P], "float32"), "YA": ("sbuf", [128, O * K], "float32"),
+    "A": ("sbuf", [128, K], "float32"), "A2": ("sbuf", [128, 2 * K], "float32"), "FA": ("sbuf", [128, K], "float32"),
+    "OG": ("sbuf", [128, 64], "float32"), "TC": ("sbuf", [128, 64], "float32"),
+    "C": ("sbuf", [128, 2 * P + 2], "float32"), "S": ("sbuf", [128, 4], "float32"), "J": ("sbuf", [128, P + 2], "float32"),
+    "zz": ("sbuf", [128, 32], "float32"), "bc": ("sbuf", [128, 64], "float32"), "RC": ("sbuf", [128, 64], "float32"),
+    "E": ("sbuf", [128, 195], "float32"), "JE": ("sbuf", [128, 130], "float32"), "Pm": ("sbuf", [128, 4], "float32"),
+    "T1": ("sbuf", [128, 4], "float32"), "T2": ("sbuf", [128, 4], "float32"),
+    "lo": ("sbuf", [128, 4], "float32"), "hi": ("sbuf", [128, 4], "float32"),
+    "pi": ("sbuf", [128, 4], "int32"), "pf": ("sbuf", [128, 4], "float32"), "gi": ("sbuf", [128, 4], "int32"), "GL": ("sbuf", [128, 4], "uint16"),
+    "PT": ("sbuf", [128, P + K * R], "float32"), "G6": ("sbuf", [128, 96], "float32"), "T6": ("sbuf", [128, 96], "float32"),
+    "D": ("sbuf", [128, 10], "float32"),
+    "p6c": ("sbuf", [128, 128], "float8_e4m3fn_x4"), "p6s": ("sbuf", [128, 128], "uint8"),
+}
+for _t in range(R):
+    SCRATCH["p%dc" % _t] = ("sbuf", [128, W[_t]], "float8_e4m3fn_x4")
+    SCRATCH["p%ds" % _t] = ("sbuf", [128, W[_t]], "uint8")
+    SCRATCH["o%dc" % _t] = ("sbuf", [128, K], "float8_e4m3fn_x4")
+    SCRATCH["o%ds" % _t] = ("sbuf", [128, K], "uint8")
+    SCRATCH["L%d" % _t] = ("sbuf", [128, 4], "uint16")
+    SCRATCH["LD%d" % _t] = ("sbuf", [128, 6], "uint16")
+    SCRATCH["LP%d" % _t] = ("sbuf", [128, 6], "uint16")
+    if _t:
+        SCRATCH["Q%d" % _t] = ("sbuf", [128, P], "float32")
+        SCRATCH["AQ%d" % _t] = ("sbuf", [128, K], "float32")
+for _b in range(8):
+    SCRATCH["b%d" % _b] = ("psum", [128, 512], "float32")
+NDMA = 22
+SEMAPHORES = ["sv", "sa", "st", "sp", "sent"] + ["arr%d" % t for t in range(R)] + ["d%d" % i for i in range(NDMA)]
+
+
+def rank_program(g, core, T, topo):
+    rank = T.rank_of(core)
+    if rank is None:
+        return
+    op_ = AluOpType
+    act = ActivationFunctionType
+    X = AxisListType.X
+    queues = {"v": g.vector, "a": g.scalar, "t": g.tensor, "p": g, "s": g.sync}
+    count = {"v": 0, "a": 0, "t": 0, "p": 0, "d": 0}
+    seen = {}
+    log = {}
+    psum = {"b%d" % b for b in range(8)}
+
+    def V(n, c0=0, c1=None, p0=0, p1=128, s=1):
+        return (n, p0, p1, c0, SCRATCH[n][1][1] if c1 is None else c1, s)
+
+    def ap(v):
+        n, p0, p1, c0, c1, s = v
+        return T[n][p0:p1, c0:c1] if s == 1 else T[n][p0:p1, c0:c1:s]
+
+    def u8(v):
+        return ap(v).bitcast(dt.uint8)
+
+    def wait(q, sem, val):
+        if seen.get((q, sem), 0) < val:
+            seen[(q, sem)] = val
+            queues[q].wait_ge(T.sem[sem], val)
+
+    def order(q, sem, val, writes, reads):
+        need = {}
+        for views, wr in ((reads, False), (writes, True)):
+            for n, p0, p1, c0, c1, s in views:
+                whole = n in psum
+                for a0, a1, b0, b1, w2, q2, sem2, val2 in log.get(n, ()):
+                    if not whole and (a1 <= p0 or p1 <= a0 or b1 <= c0 or c1 <= b0):
+                        continue
+                    if whole and q2 == q and not (w2 and not wr):
+                        continue
+                    if not whole and not (w2 or wr):
+                        continue
+                    if q2 == q and q != "s" and not w2:
+                        continue
+                    need[sem2] = max(need.get(sem2, 0), val2)
+        for s2 in sorted(need):
+            wait(q, s2, need[s2])
+        for views, wr in ((reads, False), (writes, True)):
+            for n, p0, p1, c0, c1, s in views:
+                old = log.setdefault(n, [])
+                if wr and s == 1:
+                    old[:] = [e for e in old if not (p0 <= e[0] and e[1] <= p1 and c0 <= e[2] and e[3] <= c1)]
+                old.append((p0, p1, c0, c1, wr, q, sem, val))
+
+    def op(q, writes, reads, fn):
+        count[q] += 1
+        sem = "s" + q
+        order(q, sem, count[q], writes, reads)
+        fn().then_inc(T.sem[sem], 1)
+
+    def dma(q, out, in_, rawout, rawin, writes, reads):
+        sem = "d%d" % count["d"]
+        count["d"] += 1
+        order(q, sem, 16, writes, reads)
+        queues[q].dma_start(rawout, rawin).then_inc(T.sem[sem], 16)
+
+    def ts(out, in0, s1, s2, o0, o1=None, q="v"):
+        r = [in0] + [s for s in (s1, s2) if isinstance(s, tuple)]
+        a1 = ap(s1) if isinstance(s1, tuple) else s1
+        a2 = ap(s2) if isinstance(s2, tuple) else s2
+        if o1 is None:
+            op("v", [out], r, lambda: g.vector.tensor_scalar(ap(out), ap(in0), a1, None, o0))
+        else:
+            op("v", [out], r, lambda: g.vector.tensor_scalar(ap(out), ap(in0), a1, a2, o0, o1))
+
+    def tt(out, a, b, o):
+        op("v", [out], [a, b], lambda: g.vector.tensor_tensor(ap(out), ap(a), ap(b), o))
+
+    def copy(out, a):
+        op("v", [out], [a], lambda: g.vector.tensor_copy(ap(out), ap(a)))
+
+    def gather(out, win, off):
+        op("v", [out], [win, off], lambda: g.vector.tensor_copy(ap(out), ap(win).indirect(ap(off))))
+
+    def scatter(win, off, a):
+        op("v", [win], [a, off], lambda: g.vector.tensor_copy(ap(win).indirect(ap(off)), ap(a)))
+
+    def turn(out, a):
+        op("v", [out], [a], lambda: g.vector.transpose(ap(out), ap(a)))
+
+    def fill(v, x):
+        op("v", [v], [], lambda: g.vector.memset(ap(v), x))
+
+    def sact(out, a, f):
+        op("a", [out], [a], lambda: g.scalar.activation(ap(out), ap(a), f))
+
+    def asum(out, junk, a):
+        op("a", [out, junk], [a], lambda: g.scalar.activation(ap(junk), ap(a), act.Copy, accum_out=ap(out)))
+
+    def vsum(out, a):
+        op("v", [out], [a], lambda: g.vector.tensor_reduce(ap(out), ap(a), X, op_.add))
+
+    def quant(c, s, a):
+        op("v", [c, s], [a], lambda: g.vector.quantize_mx(ap(c), ap(s), ap(a)))
+
+    def mm(bank, n, lc, ls, rc, rs):
+        out = V(bank, 0, n)
+        op("t", [out], [lc, ls, rc, rs], lambda: g.tensor.matmul_mx(ap(out), ap(lc), ap(ls), ap(rc), ap(rs), True, True))
+
+    def pick(oc, os, c, s, off):
+        op("v", [oc], [c, off], lambda: g.vector.tensor_copy(ap(oc).bitcast(dt.uint32), ap(c).bitcast(dt.uint32).indirect(ap(off))))
+        op("a", [os], [s, off], lambda: g.scalar.activation(ap(os), ap(s).indirect(ap(off)), act.Copy))
+
+    def qrep(a, b):
+        pick(V("rc", 128 * a, 128 * b), V("rs", 128 * a, 128 * b), V("qc"), V("qs"), V("qo", 8 * a, 8 * b))
+
+    dma("s", None, None, ap(V("cb")), T.c[:], [V("cb")], [])
+    dma("a", None, None, ap(V("qb")), T.qt[:], [V("qb")], [])
+    dma("s", None, None, ap(V("wb")), T.w[:], [V("wb")], [])
+    op("p", [V("pi", 0, 1)], [], lambda: g.iota(ap(V("pi", 0, 1)), [[0, 1]], 0, 1))
+    op("p", [V("gi")], [], lambda: g.iota(ap(V("gi")), [[128, 2], [16, 2]], 0, 0))
+    sl = V("C", P, P + 2)
+    op("p", [sl], [], lambda: g.iota(ap(sl), [[128, 2]], 0, 1, allow_small_or_imprecise_dtypes=True))
+    own = V("PT", 0, P)
+    op("p", [own], [], lambda: g.iota(ap(own), [[1, P]], 0, 0, allow_small_or_imprecise_dtypes=True))
+    fill(V("F"), PRED)
+    op("p", [V("F")], [V("F")], lambda: g.affine_select(ap(V("F")), ap(V("F")), [[0, 2], [-1, 128]], op_.is_gt, 1.0, 0, 1))
+    for t in range(R):
+        fill(V("qo", 8 * t, 8 * t + 8), t)
+    fill(V("zz"), 0.0)
+    fill(V("E"), 0.0)
+    ts(V("pi", 1, 2), V("pi", 0, 1), 0x6F, None, op_.bitwise_and)
+    ts(V("pi", 2, 3), V("pi", 0, 1), 0x0F, None, op_.bitwise_and)
+    copy(V("pf", 1, 3), V("pi", 1, 3))
+    ts(V("GL"), V("gi"), V("pf", 1, 2), None, op_.add)
+    span = P * RADIX - (RADIX - 1)
+    for m in range(3):
+        ts(V("lo", m, m + 1), V("pf", 2, 3), float(RADIX), float(16 * RADIX * m), op_.mult, op_.add)
+        ts(V("E", 65 * m + 64, 65 * m + 65, 0, 32), V("pf", 2, 3, 0, 32), float(-span), float(-(span * 16 * m + (RADIX - 1) * (P - 1))), op_.mult, op_.add)
+    ts(V("hi", 0, 3), V("lo", 0, 3), float(RADIX - 1), None, op_.add)
+    quant(V("qc"), V("qs"), V("qb"))
+    qrep(0, 1)
+    quant(V("p0c"), V("p0s"), V("cb"))
+
+    def rep(t):
+        return V("rc", 128 * t, 128 * t + 128), V("rs", 128 * t, 128 * t + 128)
+
+    def tile(o):
+        return V("wc", 128 * o, 128 * o + 128), V("ws", 128 * o, 128 * o + 128)
+
+    mm("b0", P, *rep(0), V("p0c"), V("p0s"))
+    sact(V("U"), V("b0", 0, P), act.Square)
+    ts(V("VZ", 0, P), V("U"), TINY, None, op_.max)
+    tt(V("VZ", P, 2 * P), V("VZ", 0, P), V("F"), op_.mult)
+
+    for t in range(R + 1):
+        if t:
+            land = [(V("p%dc" % t, K_c, K_c + K), V("p%ds" % t, K_c, K_c + K)) for K_c in [SCRATCH["p%dc" % t][1][1] - K]][0]
+            for v in land:
+                log.setdefault(v[0], []).append((0, 128, v[3], v[4], True, "net", "arr%d" % (t - 1), 16))
+            n = SCRATCH["p%dc" % t][1][1]
+            wnd = V("p%dc" % t, n - 128, n), V("p%ds" % t, n - 128, n)
+            lp = V("LP%d" % (t - 1), 0, 3)
+            if t < R:
+                mm("b0", 128, *rep(t), *wnd)
+                sact(V("A"), V("b0", 80, 128), act.Square)
+                ts(V("A2", 0, K), V("A"), TINY, None, op_.max)
+                tt(V("A2", K, 2 * K), V("A2", 0, K), V("FA"), op_.mult)
+                scatter(V("VZ"), V("LP%d" % (t - 1)), V("A2"))
+        if t < R:
+            gather(V("OG"), V("VZ", 0, P), V("GL"))
+            turn(V("TC"), V("OG"))
+            v0, v1 = V("TC", 0, 1), V("TC", 32, 33)
+            f = float(RADIX)
+            ts(V("C", 128, 256), V("VZ", 128, 256), v0, f, op_.is_lt, op_.mult)
+            ts(V("C", 0, 128), V("VZ", 256, 384), v0, f, op_.is_lt, op_.mult)
+            asum(V("S", 0, 1), V("J", 0, 257), V("C", 0, 257))
+            ts(V("C", 258, 386), V("VZ", 0, 128), v1, f, op_.is_le, op_.mult)
+            asum(V("S", 1, 2), V("J", 0, 129), V("C", 257, 386))
+            ts(V("C", 386, 514), V("VZ", 384, 512), v1, f, op_.is_lt, op_.mult)
+            vsum(V("S", 2, 3), V("C", 386, 514))
+            ts(V("bc", 0, 32), V("zz"), V("S", 0, 1), None, op_.add)
+            ts(V("bc", 32, 64), V("zz"), V("S", 2, 3), V("S", 1, 2), op_.add, op_.add)
+            turn(V("RC"), V("bc"))
+            for m in range(3):
+                ts(V("E", 65 * m, 65 * m + 64), V("RC"), V("lo", m, m + 1), V("hi", m, m + 1), op_.max, op_.min)
+                if m < 2:
+                    asum(V("Pm", m, m + 1), V("JE", 65 * m, 65 * m + 65), V("E", 65 * m, 65 * m + 65))
+            vsum(V("Pm", 2, 3), V("E", 130, 195))
+            for a in (0, 64):
+                tt(V("T1", 0, 3, a, a + 64), V("Pm", 0, 3, a, a + 64), V("Pm", 0, 3, 64 - a, 128 - a), op_.add)
+            for a in (0, 32, 64, 96):
+                b = a ^ 32
+                tt(V("T2", 0, 3, a, a + 32), V("T1", 0, 3, a, a + 32), V("T1", 0, 3, b, b + 32), op_.add)
+            lst = V("L%d" % t, 0, 3)
+            copy(lst, V("T2", 0, 3))
+            pick(V("o%dc" % t), V("o%ds" % t), V("p%dc" % t), V("p%ds" % t), lst)
+            dst = T.cores[rank ^ PART[t]]
+            rid, pid, _e = topo.addr(dst)
+            mask = sum(1 << e for e in topo.engines(core, dst)[:8])
+            n1 = SCRATCH["p%dc" % (t + 1)][1][1]
+            for x, cast in (("c", True), ("s", False)):
+                src, out = V("o%d%s" % (t, x)), V("p%d%s" % (t + 1, x), n1 - K, n1)
+                order("p", "sent", 0, [], [src])
+                g.remote_dma(u8(out) if cast else ap(out), u8(src) if cast else ap(src), T.sem["arr%d" % t], T.sem["sent"], pid, rid, mask)
+            if t < R - 1:
+                for x in "cs":
+                    a, b = V("p%d%s" % (t, x)), V("p%d%s" % (t + 1, x), 0, W[t])
+                    dma("s", None, None, u8(b) if x == "c" else ap(b), u8(a) if x == "c" else ap(a), [b], [a])
+            elif t == R - 1:
+                for x in "cs":
+                    a, b = V("p%d%s" % (t, x), 0, 80), V("p%d%s" % (t + 1, x), 0, 80)
+                    dma("s", None, None, u8(b) if x == "c" else ap(b), u8(a) if x == "c" else ap(a), [b], [a])
+            if t == 0:
+                qrep(1, 2)
+                mm("b1", P, *rep(1), V("p0c"), V("p0s"))
+                sact(V("Q1"), V("b1", 0, P), act.Square)
+            ld = "LD%d" % t
+            copy(V(ld, 0, 6, s=2), V("T2", 0, 3))
+            copy(V(ld, 1, 6, s=2), V("T2", 0, 3))
+            gather(V("G6"), V("PT", 0, W[t]), V(ld))
+            turn(V("T6"), V("G6"))
+            copy(V("LP%d" % t, 0, 3), V("T6", 0, 96, s=32))
+            ts(V("LP%d" % t, 3, 6), V("T6", 0, 96, s=32), float(P), None, op_.add)
+        if t and t < R:
+            scatter(V("U"), lp, V("A"))
+        if t and t + 1 < R:
+            for t2 in range(t + 1, R):
+                b = "b%d" % (t2 - t)
+                mm(b, 128, *rep(t2), *wnd)
+                sact(V("AQ%d" % t2), V(b, 80, 128), act.Square)
+            scatter(V("Q%d" % (t + 1)), lp, V("AQ%d" % (t + 1)))
+        if t + 1 < R:
+            gather(V("FA"), V("F"), V("LP%d" % t, 0, 3))
+            tt(V("U"), V("U"), V("Q%d" % (t + 1)), op_.add)
+            ts(V("VZ", 0, P), V("U"), TINY, None, op_.max)
+            tt(V("VZ", P, 2 * P), V("VZ", 0, P), V("F"), op_.mult)
+            gather(V("PT", W[t], W[t] + K), V("PT", 0, W[t]), V("L%d" % t, 0, 3))
+            code = V("bc", 0, 64, s=32)
+            tt(V("D", 0, 2), code, sl, op_.subtract)
+            ts(V("D", 2, 4), V("D", 0, 2), 1.0 / RADIX, float(W[t]), op_.mult, op_.add)
+            ts(V("D", 4, 6), V("D", 0, 2), float(RADIX * K), None, op_.is_lt)
+            tt(V("D", 6, 8), V("D", 2, 4), sl, op_.subtract)
+            tt(V("D", 8, 10), V("D", 6, 8), V("D", 4, 6), op_.mult)
+            tt(sl, sl, V("D", 8, 10), op_.add)
+        if t == 0:
+            quant(V("wc"), V("ws"), V("wb"))
+            qrep(2, R)
+            for t2 in range(2, R):
+                b = "b%d" % t2
+                mm(b, P, *rep(t2), V("p0c"), V("p0s"))
+                sact(V("Q%d" % t2), V(b, 0, P), act.Square)
+            for o in range(O):
+                b = "b%d" % (6 + o)
+                mm(b, P, *tile(o), V("p0c"), V("p0s"))
+                sact(V("Y", P * o, P * o + P), V(b, 0, P), act.Copy)
+        else:
+            for t2 in range(t + 2, R):
+                scatter(V("Q%d" % t2), lp, V("AQ%d" % t2))
+            for o in range(O):
+                b = "b%d" % (6 + o)
+                mm(b, 128, *tile(o), *wnd)
+                sact(V("YA", K * o, K * o + K), V(b, 80, 128), act.Copy)
+                scatter(V("Y", P * o, P * o + P), lp, V("YA", K * o, K * o + K))
+            w = O * P
+            dma("s", None, None, T.y[:, (t - 1) * w:t * w], ap(V("Y")), [], [V("Y")])
+
+    for q in "vatp":
+        wait("p", "s" + q, count[q])
+    for i in range(count["d"]):
+        wait("p", "d%d" % i, 16)
+    for t in range(R):
+        wait("p", "arr%d" % t, 16)
+    wait("p", "sent", 16 * R)

@@ -1,10 +1,13 @@
+from concourse.bass import DstId, RemoteDMATransfer
 from concourse.mybir import dt, AluOpType, AxisListType, ActivationFunctionType
 
 N, P, K, R, O = 8, 256, 48, 6, 2
 PART = [1, 2, 4, 1, 2, 4]
+NE = 8
 W = [P + K * t for t in range(R)]
 PRED = 1.0 - 2.0 ** -24
 TINY = 2.0 ** -122
+PAD = 3 * K
 RADIX = 512
 
 SCRATCH = {
@@ -24,14 +27,15 @@ SCRATCH = {
     "lo": ("sbuf", [128, 4], "float32"), "hi": ("sbuf", [128, 4], "float32"),
     "pi": ("sbuf", [128, 4], "int32"), "pf": ("sbuf", [128, 4], "float32"), "gi": ("sbuf", [128, 4], "int32"), "GL": ("sbuf", [128, 4], "uint16"),
     "PT": ("sbuf", [128, P + K * R], "float32"), "G6": ("sbuf", [128, 96], "float32"), "T6": ("sbuf", [128, 96], "float32"),
-    "D": ("sbuf", [128, 10], "float32"),
-    "p6c": ("sbuf", [128, 128], "float8_e4m3fn_x4"), "p6s": ("sbuf", [128, 128], "uint8"),
+    "D": ("sbuf", [128, 8], "float32"), "vc": ("sbuf", [128, 2], "float32"), "pl": ("sbuf", [128, 2], "float32"),
+    "EK": ("sbuf", [128, 2 * K], "float32"), "EP": ("sbuf", [128, 2 * K + 2], "float32"),
+    "p6c": ("sbuf", [128, 128], "float8_e4m3fn_x4"), "p6s": ("sbuf", [128, 128 + PAD], "uint8"),
 }
 for _t in range(R):
     SCRATCH["p%dc" % _t] = ("sbuf", [128, W[_t]], "float8_e4m3fn_x4")
-    SCRATCH["p%ds" % _t] = ("sbuf", [128, W[_t]], "uint8")
+    SCRATCH["p%ds" % _t] = ("sbuf", [128, W[_t] + PAD], "uint8")
     SCRATCH["o%dc" % _t] = ("sbuf", [128, K], "float8_e4m3fn_x4")
-    SCRATCH["o%ds" % _t] = ("sbuf", [128, K], "uint8")
+    SCRATCH["o%ds" % _t] = ("sbuf", [128, K + PAD], "uint8")
     SCRATCH["L%d" % _t] = ("sbuf", [128, 4], "uint16")
     SCRATCH["LD%d" % _t] = ("sbuf", [128, 6], "uint16")
     SCRATCH["LP%d" % _t] = ("sbuf", [128, 6], "uint16")
@@ -40,7 +44,7 @@ for _t in range(R):
         SCRATCH["AQ%d" % _t] = ("sbuf", [128, K], "float32")
 for _b in range(8):
     SCRATCH["b%d" % _b] = ("psum", [128, 512], "float32")
-NDMA = 22
+NDMA = 28
 SEMAPHORES = ["sv", "sa", "st", "sp", "sent"] + ["arr%d" % t for t in range(R)] + ["d%d" % i for i in range(NDMA)]
 
 
@@ -102,13 +106,13 @@ def rank_program(g, core, T, topo):
         order(q, sem, count[q], writes, reads)
         fn().then_inc(T.sem[sem], 1)
 
-    def dma(q, out, in_, rawout, rawin, writes, reads):
+    def dma(q, out, in_, writes, reads):
         sem = "d%d" % count["d"]
         count["d"] += 1
-        order(q, sem, 16, writes, reads)
-        queues[q].dma_start(rawout, rawin).then_inc(T.sem[sem], 16)
+        order("d" + q if False else q, sem, 16, writes, reads)
+        queues[q].dma_start(out, in_).then_inc(T.sem[sem], 16)
 
-    def ts(out, in0, s1, s2, o0, o1=None, q="v"):
+    def ts(out, in0, s1, s2, o0, o1=None):
         r = [in0] + [s for s in (s1, s2) if isinstance(s, tuple)]
         a1 = ap(s1) if isinstance(s1, tuple) else s1
         a2 = ap(s2) if isinstance(s2, tuple) else s2
@@ -141,8 +145,8 @@ def rank_program(g, core, T, topo):
     def asum(out, junk, a):
         op("a", [out, junk], [a], lambda: g.scalar.activation(ap(junk), ap(a), act.Copy, accum_out=ap(out)))
 
-    def vsum(out, a):
-        op("v", [out], [a], lambda: g.vector.tensor_reduce(ap(out), ap(a), X, op_.add))
+    def vsum(out, a, o=op_.add):
+        op("v", [out], [a], lambda: g.vector.tensor_reduce(ap(out), ap(a), X, o))
 
     def quant(c, s, a):
         op("v", [c, s], [a], lambda: g.vector.quantize_mx(ap(c), ap(s), ap(a)))
@@ -158,15 +162,25 @@ def rank_program(g, core, T, topo):
     def qrep(a, b):
         pick(V("rc", 128 * a, 128 * b), V("rs", 128 * a, 128 * b), V("qc"), V("qs"), V("qo", 8 * a, 8 * b))
 
-    dma("s", None, None, ap(V("cb")), T.c[:], [V("cb")], [])
-    dma("a", None, None, ap(V("qb")), T.qt[:], [V("qb")], [])
-    dma("s", None, None, ap(V("wb")), T.w[:], [V("wb")], [])
-    op("p", [V("pi", 0, 1)], [], lambda: g.iota(ap(V("pi", 0, 1)), [[0, 1]], 0, 1))
-    op("p", [V("gi")], [], lambda: g.iota(ap(V("gi")), [[128, 2], [16, 2]], 0, 0))
+    def rep(t):
+        return V("rc", 128 * t, 128 * t + 128), V("rs", 128 * t, 128 * t + 128)
+
+    def tile(o):
+        return V("wc", 128 * o, 128 * o + 128), V("ws", 128 * o, 128 * o + 128)
+
+    def whole(v, out, **k):
+        op("p", [v], [], lambda: g.iota(ap(v), *out, **k))
+
+    dma("s", ap(V("cb")), T.c[:], [V("cb")], [])
+    dma("a", ap(V("qb")), T.qt[:], [V("qb")], [])
+    dma("s", ap(V("wb")), T.w[:], [V("wb")], [])
     sl = V("C", P, P + 2)
-    op("p", [sl], [], lambda: g.iota(ap(sl), [[128, 2]], 0, 1, allow_small_or_imprecise_dtypes=True))
-    own = V("PT", 0, P)
-    op("p", [own], [], lambda: g.iota(ap(own), [[1, P]], 0, 0, allow_small_or_imprecise_dtypes=True))
+    fl = {"allow_small_or_imprecise_dtypes": True}
+    whole(V("pi", 0, 1), ([[0, 1]], 0, 1))
+    whole(V("gi"), ([[128, 2], [16, 2]], 0, 0))
+    whole(sl, ([[128, 2]], 0, 1), **fl)
+    whole(V("pl"), ([[128, 2]], 0, 1), **fl)
+    whole(V("PT", 0, P), ([[1, P]], 0, 0), **fl)
     fill(V("F"), PRED)
     op("p", [V("F")], [V("F")], lambda: g.affine_select(ap(V("F")), ap(V("F")), [[0, 2], [-1, 128]], op_.is_gt, 1.0, 0, 1))
     for t in range(R):
@@ -184,43 +198,49 @@ def rank_program(g, core, T, topo):
     ts(V("hi", 0, 3), V("lo", 0, 3), float(RADIX - 1), None, op_.add)
     quant(V("qc"), V("qs"), V("qb"))
     qrep(0, 1)
-    quant(V("p0c"), V("p0s"), V("cb"))
+    own = V("p0c"), V("p0s", 0, P)
+    quant(*own, V("cb"))
 
-    def rep(t):
-        return V("rc", 128 * t, 128 * t + 128), V("rs", 128 * t, 128 * t + 128)
-
-    def tile(o):
-        return V("wc", 128 * o, 128 * o + 128), V("ws", 128 * o, 128 * o + 128)
-
-    mm("b0", P, *rep(0), V("p0c"), V("p0s"))
+    mm("b0", P, *rep(0), *own)
+    for x in range(2):
+        mm("b%d" % (6 + x), 128, V("p0c", 128 * x, 128 * x + 128), V("p0s", 128 * x, 128 * x + 128), V("qc"), V("qs"))
     sact(V("U"), V("b0", 0, P), act.Square)
+    for x in range(2):
+        s0 = V("b%d" % (6 + x), 0, 1)
+        ts(V("vc", x, x + 1), s0, s0, TINY, op_.mult, op_.max)
     ts(V("VZ", 0, P), V("U"), TINY, None, op_.max)
-    tt(V("VZ", P, 2 * P), V("VZ", 0, P), V("F"), op_.mult)
 
     for t in range(R + 1):
+        more = t + 1 < R
         if t:
-            land = [(V("p%dc" % t, K_c, K_c + K), V("p%ds" % t, K_c, K_c + K)) for K_c in [SCRATCH["p%dc" % t][1][1] - K]][0]
-            for v in land:
-                log.setdefault(v[0], []).append((0, 128, v[3], v[4], True, "net", "arr%d" % (t - 1), 16))
-            n = SCRATCH["p%dc" % t][1][1]
+            n = W[t] if t < R else 128
+            log.setdefault("p%dc" % t, []).append((0, 128, n - K, n, True, "net", "arr%d" % (t - 1), NE))
+            log.setdefault("p%ds" % t, []).append((0, 128, n - K, n + PAD, True, "net", "arr%d" % (t - 1), NE))
             wnd = V("p%dc" % t, n - 128, n), V("p%ds" % t, n - 128, n)
             lp = V("LP%d" % (t - 1), 0, 3)
             if t < R:
                 mm("b0", 128, *rep(t), *wnd)
                 sact(V("A"), V("b0", 80, 128), act.Square)
+                tt(V("EP", 0, K), V("EK", 0, K), V("A"), op_.mult)
+                tt(V("EP", K + 1, 2 * K + 1), V("EK", K, 2 * K), V("A"), op_.mult)
                 ts(V("A2", 0, K), V("A"), TINY, None, op_.max)
+                vsum(V("vc", 0, 1), V("EP", 0, K + 1), op_.max)
                 tt(V("A2", K, 2 * K), V("A2", 0, K), V("FA"), op_.mult)
+                vsum(V("vc", 1, 2), V("EP", K + 1, 2 * K + 2), op_.max)
                 scatter(V("VZ"), V("LP%d" % (t - 1)), V("A2"))
         if t < R:
-            gather(V("OG"), V("VZ", 0, P), V("GL"))
-            turn(V("TC"), V("OG"))
-            v0, v1 = V("TC", 0, 1), V("TC", 32, 33)
+            v0, v1 = V("vc", 0, 1), V("vc", 1, 2)
             f = float(RADIX)
             ts(V("C", 128, 256), V("VZ", 128, 256), v0, f, op_.is_lt, op_.mult)
-            ts(V("C", 0, 128), V("VZ", 256, 384), v0, f, op_.is_lt, op_.mult)
-            asum(V("S", 0, 1), V("J", 0, 257), V("C", 0, 257))
-            ts(V("C", 258, 386), V("VZ", 0, 128), v1, f, op_.is_le, op_.mult)
-            asum(V("S", 1, 2), V("J", 0, 129), V("C", 257, 386))
+            for half in ((0, 1) if t else (1, 0)):
+                if half:
+                    ts(V("C", 258, 386), V("VZ", 0, 128), v1, f, op_.is_le, op_.mult)
+                    asum(V("S", 1, 2), V("J", 0, 129), V("C", 257, 386))
+                    if not t:
+                        tt(V("VZ", P, 2 * P), V("VZ", 0, P), V("F"), op_.mult)
+                else:
+                    ts(V("C", 0, 128), V("VZ", 256, 384), v0, f, op_.is_lt, op_.mult)
+                    asum(V("S", 0, 1), V("J", 0, 257), V("C", 0, 257))
             ts(V("C", 386, 514), V("VZ", 384, 512), v1, f, op_.is_lt, op_.mult)
             vsum(V("S", 2, 3), V("C", 386, 514))
             ts(V("bc", 0, 32), V("zz"), V("S", 0, 1), None, op_.add)
@@ -238,65 +258,76 @@ def rank_program(g, core, T, topo):
                 tt(V("T2", 0, 3, a, a + 32), V("T1", 0, 3, a, a + 32), V("T1", 0, 3, b, b + 32), op_.add)
             lst = V("L%d" % t, 0, 3)
             copy(lst, V("T2", 0, 3))
-            pick(V("o%dc" % t), V("o%ds" % t), V("p%dc" % t), V("p%ds" % t), lst)
+            pick(V("o%dc" % t), V("o%ds" % t, 0, K), V("p%dc" % t), V("p%ds" % t, 0, W[t]), lst)
+            if t == 0:
+                for t2 in range(R):
+                    v = V("o%ds" % t2, K, K + PAD)
+                    dma("s", ap(v), ap(V("p0s", 0, PAD)), [v], [V("p0s", 0, PAD)])
             dst = T.cores[rank ^ PART[t]]
             rid, pid, _e = topo.addr(dst)
-            mask = sum(1 << e for e in topo.engines(core, dst)[:8])
-            n1 = SCRATCH["p%dc" % (t + 1)][1][1]
-            for x, cast in (("c", True), ("s", False)):
-                src, out = V("o%d%s" % (t, x)), V("p%d%s" % (t + 1, x), n1 - K, n1)
-                order("p", "sent", 0, [], [src])
-                g.remote_dma(u8(out) if cast else ap(out), u8(src) if cast else ap(src), T.sem["arr%d" % t], T.sem["sent"], pid, rid, mask)
-            if t < R - 1:
-                for x in "cs":
-                    a, b = V("p%d%s" % (t, x)), V("p%d%s" % (t + 1, x), 0, W[t])
-                    dma("s", None, None, u8(b) if x == "c" else ap(b), u8(a) if x == "c" else ap(a), [b], [a])
-            elif t == R - 1:
-                for x in "cs":
-                    a, b = V("p%d%s" % (t, x), 0, 80), V("p%d%s" % (t + 1, x), 0, 80)
-                    dma("s", None, None, u8(b) if x == "c" else ap(b), u8(a) if x == "c" else ap(a), [b], [a])
+            engs = topo.engines(core, dst)[:NE]
+            n1 = W[t + 1] if more else 128
+            order("p", "sent", 0, [], [V("o%dc" % t), V("o%ds" % t)])
+            g.remote_dma_fused([
+                RemoteDMATransfer(dst_ids=[DstId(rid=rid, pnc=pid)], dma_engine_mask=sum(1 << e for e in es), remote_sem=T.sem["arr%d" % t], src=src, dst=out)
+                for es, src, out in (
+                    (engs[0::2], u8(V("o%dc" % t)), u8(V("p%dc" % (t + 1), n1 - K, n1))),
+                    (engs[1::2], ap(V("o%ds" % t)), ap(V("p%ds" % (t + 1), n1 - K, n1 + PAD))))], local_sem=T.sem["sent"])
+            n2 = W[t] if more else 80
+            for x in "cs":
+                a, b = V("p%d%s" % (t, x), 0, n2), V("p%d%s" % (t + 1, x), 0, n2)
+                dma("s", u8(b) if x == "c" else ap(b), u8(a) if x == "c" else ap(a), [b], [a])
             if t == 0:
                 qrep(1, 2)
-                mm("b1", P, *rep(1), V("p0c"), V("p0s"))
+                mm("b1", P, *rep(1), *own)
                 sact(V("Q1"), V("b1", 0, P), act.Square)
             ld = "LD%d" % t
+            D0, D1, D2, D3 = V("D", 0, 2), V("D", 2, 4), V("D", 4, 6), V("D", 6, 8)
+            new = V("PT", W[t], W[t] + K)
             copy(V(ld, 0, 6, s=2), V("T2", 0, 3))
             copy(V(ld, 1, 6, s=2), V("T2", 0, 3))
+            if more:
+                tt(D0, V("bc", 0, 64, s=32), sl, op_.subtract)
             gather(V("G6"), V("PT", 0, W[t]), V(ld))
+            if more:
+                ts(D1, D0, 1.0 / RADIX, float(W[t]), op_.mult, op_.add)
+                ts(D2, D0, float(RADIX * K), None, op_.is_ge)
             turn(V("T6"), V("G6"))
+            if more:
+                gather(new, V("PT", 0, W[t]), lst)
+                tt(D3, sl, D1, op_.subtract)
             copy(V("LP%d" % t, 0, 3), V("T6", 0, 96, s=32))
             ts(V("LP%d" % t, 3, 6), V("T6", 0, 96, s=32), float(P), None, op_.add)
-        if t and t < R:
+        if t and more:
             scatter(V("U"), lp, V("A"))
-        if t and t + 1 < R:
             for t2 in range(t + 1, R):
                 b = "b%d" % (t2 - t)
                 mm(b, 128, *rep(t2), *wnd)
                 sact(V("AQ%d" % t2), V(b, 80, 128), act.Square)
             scatter(V("Q%d" % (t + 1)), lp, V("AQ%d" % (t + 1)))
-        if t + 1 < R:
+        if more:
+            tt(D3, D3, D2, op_.mult)
             gather(V("FA"), V("F"), V("LP%d" % t, 0, 3))
             tt(V("U"), V("U"), V("Q%d" % (t + 1)), op_.add)
+            tt(sl, D1, D3, op_.add)
             ts(V("VZ", 0, P), V("U"), TINY, None, op_.max)
+            ts(V("EK", 0, K), new, V("pl", 0, 1), None, op_.is_equal)
+            ts(V("EK", K, 2 * K), new, V("pl", 1, 2), None, op_.is_equal)
             tt(V("VZ", P, 2 * P), V("VZ", 0, P), V("F"), op_.mult)
-            gather(V("PT", W[t], W[t] + K), V("PT", 0, W[t]), V("L%d" % t, 0, 3))
-            code = V("bc", 0, 64, s=32)
-            tt(V("D", 0, 2), code, sl, op_.subtract)
-            ts(V("D", 2, 4), V("D", 0, 2), 1.0 / RADIX, float(W[t]), op_.mult, op_.add)
-            ts(V("D", 4, 6), V("D", 0, 2), float(RADIX * K), None, op_.is_lt)
-            tt(V("D", 6, 8), V("D", 2, 4), sl, op_.subtract)
-            tt(V("D", 8, 10), V("D", 6, 8), V("D", 4, 6), op_.mult)
-            tt(sl, sl, V("D", 8, 10), op_.add)
+            gather(V("OG"), V("VZ", 0, P), V("GL"))
+            turn(V("TC"), V("OG"))
+            for x in range(2):
+                ts(V("EP", 49 * x + K, 49 * x + K + 1), V("TC", 32 * x, 32 * x + 1), V("D", 4 + x, 5 + x), TINY, op_.mult, op_.max)
         if t == 0:
             quant(V("wc"), V("ws"), V("wb"))
             qrep(2, R)
             for t2 in range(2, R):
                 b = "b%d" % t2
-                mm(b, P, *rep(t2), V("p0c"), V("p0s"))
+                mm(b, P, *rep(t2), *own)
                 sact(V("Q%d" % t2), V(b, 0, P), act.Square)
             for o in range(O):
                 b = "b%d" % (6 + o)
-                mm(b, P, *tile(o), V("p0c"), V("p0s"))
+                mm(b, P, *tile(o), *own)
                 sact(V("Y", P * o, P * o + P), V(b, 0, P), act.Copy)
         else:
             for t2 in range(t + 2, R):
@@ -306,13 +337,16 @@ def rank_program(g, core, T, topo):
                 mm(b, 128, *tile(o), *wnd)
                 sact(V("YA", K * o, K * o + K), V(b, 80, 128), act.Copy)
                 scatter(V("Y", P * o, P * o + P), lp, V("YA", K * o, K * o + K))
-            w = O * P
-            dma("s", None, None, T.y[:, (t - 1) * w:t * w], ap(V("Y")), [], [V("Y")])
+                if t == R:
+                    i = ((t - 1) * O + o) * P
+                    dma("sa"[o], T.y[:, i:i + P], ap(V("Y", P * o, P * o + P)), [], [V("Y", P * o, P * o + P)])
+            if t < R:
+                dma("s", T.y[:, (t - 1) * O * P:t * O * P], ap(V("Y")), [], [V("Y")])
 
     for q in "vatp":
         wait("p", "s" + q, count[q])
     for i in range(count["d"]):
         wait("p", "d%d" % i, 16)
     for t in range(R):
-        wait("p", "arr%d" % t, 16)
-    wait("p", "sent", 16 * R)
+        wait("p", "arr%d" % t, NE)
+    wait("p", "sent", NE * R)

@@ -10,40 +10,24 @@ TINY = 2.0 ** -122
 PAD = 3 * K
 RADIX = 512
 
-SCRATCH = {
-    "cb": ("sbuf", [128, 4 * P], "bfloat16"), "qb": ("sbuf", [128, 512], "bfloat16"), "wb": ("sbuf", [128, 512 * O], "bfloat16"),
-    "qc": ("sbuf", [128, 128], "float8_e4m3fn_x4"), "qs": ("sbuf", [128, 128], "uint8"),
-    "rc": ("sbuf", [128, 128 * R], "float8_e4m3fn_x4"), "rs": ("sbuf", [128, 128 * R], "uint8"),
-    "wc": ("sbuf", [128, 128 * O], "float8_e4m3fn_x4"), "ws": ("sbuf", [128, 128 * O], "uint8"),
-    "qo": ("sbuf", [128, 8 * R], "uint16"),
-    "VZ": ("sbuf", [128, 2 * P], "float32"), "U": ("sbuf", [128, P], "float32"), "F": ("sbuf", [128, P], "float32"),
-    "Y": ("sbuf", [128, O * P], "float32"), "YA": ("sbuf", [128, O * K], "float32"),
-    "A": ("sbuf", [128, K], "float32"), "A2": ("sbuf", [128, 2 * K], "float32"), "FA": ("sbuf", [128, K], "float32"),
-    "OG": ("sbuf", [128, 64], "float32"), "TC": ("sbuf", [128, 64], "float32"),
-    "C": ("sbuf", [128, 2 * P + 2], "float32"), "S": ("sbuf", [128, 4], "float32"), "J": ("sbuf", [128, P + 2], "float32"),
-    "zz": ("sbuf", [128, 32], "float32"), "bc": ("sbuf", [128, 64], "float32"), "RC": ("sbuf", [128, 64], "float32"),
-    "E": ("sbuf", [128, 195], "float32"), "JE": ("sbuf", [128, 130], "float32"), "Pm": ("sbuf", [128, 4], "float32"),
-    "T1": ("sbuf", [128, 4], "float32"), "T2": ("sbuf", [128, 4], "float32"),
-    "lo": ("sbuf", [128, 4], "float32"), "hi": ("sbuf", [128, 4], "float32"),
-    "pi": ("sbuf", [128, 4], "int32"), "pf": ("sbuf", [128, 4], "float32"), "gi": ("sbuf", [128, 4], "int32"), "GL": ("sbuf", [128, 4], "uint16"),
-    "PT": ("sbuf", [128, P + K * R], "float32"), "G6": ("sbuf", [128, 96], "float32"), "T6": ("sbuf", [128, 96], "float32"),
-    "D": ("sbuf", [128, 8], "float32"), "vc": ("sbuf", [128, 2], "float32"), "pl": ("sbuf", [128, 2], "float32"),
-    "EK": ("sbuf", [128, 2 * K], "float32"), "EP": ("sbuf", [128, 2 * K + 2], "float32"),
-    "p6c": ("sbuf", [128, 128], "float8_e4m3fn_x4"), "p6s": ("sbuf", [128, 128 + PAD], "uint8"),
-}
+F32, CODE, U8, U16, BF = "float32", "float8_e4m3fn_x4", "uint8", "uint16", "bfloat16"
+SCRATCH = {n: ("sbuf", [128, w], d) for n, w, d in (
+    ("cb", 4 * P, BF), ("qb", 512, BF), ("wb", 512 * O, BF),
+    ("qc", 128, CODE), ("qs", 128, U8), ("rc", 128 * R, CODE), ("rs", 128 * R, U8), ("wc", 128 * O, CODE), ("ws", 128 * O, U8),
+    ("VZ", 2 * P, F32), ("U", P, F32), ("F", P, F32), ("A", K, F32), ("A2", K, F32), ("FX", 2 * K, F32), ("ZA", 2 * K, F32),
+    ("EK", 2 * K, F32), ("EP", 2 * K + 2, F32), ("vc", 2, F32), ("pl", 2, F32), ("OG", 64, F32), ("TC", 64, F32), ("big", K, F32),
+    ("C", 2 * (P + K + 1), F32), ("S", 4, F32), ("J", P, F32), ("JS", 177, F32), ("zz", 32, F32), ("bc", 64, F32), ("RC", 64, F32),
+    ("E", 195, F32), ("JE", 130, F32), ("Pm", 4, F32), ("T1", 4, F32), ("T2", 4, F32), ("lo", 4, F32), ("hi", 4, F32),
+    ("pi", 4, "int32"), ("gi", 4, "int32"), ("pf", 4, F32), ("GL", 4, U16), ("du", 6, U16), ("qo", 8 * R, U16),
+    ("PT", P + K * R, F32), ("G6", 96, F32), ("T6", 96, F32), ("D", 8, F32),
+    ("Y", O * P, F32), ("YA", O * K, F32), ("p6c", 128, CODE), ("p6s", 128 + PAD, U8))}
 for _t in range(R):
-    SCRATCH["p%dc" % _t] = ("sbuf", [128, W[_t]], "float8_e4m3fn_x4")
-    SCRATCH["p%ds" % _t] = ("sbuf", [128, W[_t] + PAD], "uint8")
-    SCRATCH["o%dc" % _t] = ("sbuf", [128, K], "float8_e4m3fn_x4")
-    SCRATCH["o%ds" % _t] = ("sbuf", [128, K + PAD], "uint8")
-    SCRATCH["L%d" % _t] = ("sbuf", [128, 4], "uint16")
-    SCRATCH["LD%d" % _t] = ("sbuf", [128, 6], "uint16")
-    SCRATCH["LP%d" % _t] = ("sbuf", [128, 6], "uint16")
-    if _t:
-        SCRATCH["Q%d" % _t] = ("sbuf", [128, P], "float32")
-        SCRATCH["AQ%d" % _t] = ("sbuf", [128, K], "float32")
+    for _n, _w, _d in (("p%dc", W[_t], CODE), ("p%ds", W[_t] + PAD, U8), ("o%dc", K, CODE), ("o%ds", K + PAD, U8),
+                       ("L%d", 4, U16), ("LP%d", 4, U16), ("Q%d", P, F32), ("AQ%d", K, F32)):
+        if _t or _d != F32:
+            SCRATCH[_n % _t] = ("sbuf", [128, _w], _d)
 for _b in range(8):
-    SCRATCH["b%d" % _b] = ("psum", [128, 512], "float32")
+    SCRATCH["b%d" % _b] = ("psum", [128, 512], F32)
 NDMA = 28
 SEMAPHORES = ["sv", "sa", "st", "sp", "sent"] + ["arr%d" % t for t in range(R)] + ["d%d" % i for i in range(NDMA)]
 
@@ -109,7 +93,7 @@ def rank_program(g, core, T, topo):
     def dma(q, out, in_, writes, reads):
         sem = "d%d" % count["d"]
         count["d"] += 1
-        order("d" + q if False else q, sem, 16, writes, reads)
+        order(q, sem, 16, writes, reads)
         queues[q].dma_start(out, in_).then_inc(T.sem[sem], 16)
 
     def ts(out, in0, s1, s2, o0, o1=None):
@@ -174,7 +158,9 @@ def rank_program(g, core, T, topo):
     dma("s", ap(V("cb")), T.c[:], [V("cb")], [])
     dma("a", ap(V("qb")), T.qt[:], [V("qb")], [])
     dma("s", ap(V("wb")), T.w[:], [V("wb")], [])
-    sl = V("C", P, P + 2)
+    c0lo, c0hi, c0ar = V("C", 0, 128), V("C", 128, 256), V("C", 256, 304)
+    sl = V("C", 304, 306)
+    c1ar, c1lo, c1hi = V("C", 306, 354), V("C", 354, 482), V("C", 482, 610)
     fl = {"allow_small_or_imprecise_dtypes": True}
     whole(V("pi", 0, 1), ([[0, 1]], 0, 1))
     whole(V("gi"), ([[128, 2], [16, 2]], 0, 0))
@@ -187,14 +173,20 @@ def rank_program(g, core, T, topo):
         fill(V("qo", 8 * t, 8 * t + 8), t)
     fill(V("zz"), 0.0)
     fill(V("E"), 0.0)
+    fill(c0ar, 0.0)
+    fill(c1ar, 0.0)
+    fill(V("big"), 1e29)
     ts(V("pi", 1, 2), V("pi", 0, 1), 0x6F, None, op_.bitwise_and)
     ts(V("pi", 2, 3), V("pi", 0, 1), 0x0F, None, op_.bitwise_and)
     copy(V("pf", 1, 3), V("pi", 1, 3))
     ts(V("GL"), V("gi"), V("pf", 1, 2), None, op_.add)
+    ts(V("big"), V("big"), 1e9, None, op_.mult)
     span = P * RADIX - (RADIX - 1)
     for m in range(3):
         ts(V("lo", m, m + 1), V("pf", 2, 3), float(RADIX), float(16 * RADIX * m), op_.mult, op_.add)
         ts(V("E", 65 * m + 64, 65 * m + 65, 0, 32), V("pf", 2, 3, 0, 32), float(-span), float(-(span * 16 * m + (RADIX - 1) * (P - 1))), op_.mult, op_.add)
+        for j in (2 * m, 2 * m + 1):
+            ts(V("du", j, j + 1), V("pf", 2, 3), float(16 * m), None, op_.add)
     ts(V("hi", 0, 3), V("lo", 0, 3), float(RADIX - 1), None, op_.add)
     quant(V("qc"), V("qs"), V("qb"))
     qrep(0, 1)
@@ -204,11 +196,13 @@ def rank_program(g, core, T, topo):
     mm("b0", P, *rep(0), *own)
     for x in range(2):
         mm("b%d" % (6 + x), 128, V("p0c", 128 * x, 128 * x + 128), V("p0s", 128 * x, 128 * x + 128), V("qc"), V("qs"))
-    sact(V("U"), V("b0", 0, P), act.Square)
+    for x in (1, 0):
+        sact(V("U", 128 * x, 128 * x + 128), V("b0", 128 * x, 128 * x + 128), act.Square)
     for x in range(2):
         s0 = V("b%d" % (6 + x), 0, 1)
         ts(V("vc", x, x + 1), s0, s0, TINY, op_.mult, op_.max)
-    ts(V("VZ", 0, P), V("U"), TINY, None, op_.max)
+    for x in (1, 0):
+        ts(V("VZ", 128 * x, 128 * x + 128), V("U", 128 * x, 128 * x + 128), TINY, None, op_.max)
 
     for t in range(R + 1):
         more = t + 1 < R
@@ -223,27 +217,42 @@ def rank_program(g, core, T, topo):
                 sact(V("A"), V("b0", 80, 128), act.Square)
                 tt(V("EP", 0, K), V("EK", 0, K), V("A"), op_.mult)
                 tt(V("EP", K + 1, 2 * K + 1), V("EK", K, 2 * K), V("A"), op_.mult)
-                ts(V("A2", 0, K), V("A"), TINY, None, op_.max)
+                ts(V("A2"), V("A"), TINY, None, op_.max)
                 vsum(V("vc", 0, 1), V("EP", 0, K + 1), op_.max)
-                tt(V("A2", K, 2 * K), V("A2", 0, K), V("FA"), op_.mult)
                 vsum(V("vc", 1, 2), V("EP", K + 1, 2 * K + 2), op_.max)
-                scatter(V("VZ"), V("LP%d" % (t - 1)), V("A2"))
+                for x in range(2):
+                    tt(V("ZA", K * x, K * x + K), V("A2"), V("FX", K * x, K * x + K), op_.mult)
         if t < R:
             v0, v1 = V("vc", 0, 1), V("vc", 1, 2)
             f = float(RADIX)
-            ts(V("C", 128, 256), V("VZ", 128, 256), v0, f, op_.is_lt, op_.mult)
-            for half in ((0, 1) if t else (1, 0)):
-                if half:
-                    ts(V("C", 258, 386), V("VZ", 0, 128), v1, f, op_.is_le, op_.mult)
-                    asum(V("S", 1, 2), V("J", 0, 129), V("C", 257, 386))
-                    if not t:
-                        tt(V("VZ", P, 2 * P), V("VZ", 0, P), V("F"), op_.mult)
-                else:
-                    ts(V("C", 0, 128), V("VZ", 256, 384), v0, f, op_.is_lt, op_.mult)
-                    asum(V("S", 0, 1), V("J", 0, 257), V("C", 0, 257))
-            ts(V("C", 386, 514), V("VZ", 384, 512), v1, f, op_.is_lt, op_.mult)
-            vsum(V("S", 2, 3), V("C", 386, 514))
-            ts(V("bc", 0, 32), V("zz"), V("S", 0, 1), None, op_.add)
+
+            def x0lo():
+                ts(c0lo, V("VZ", 256, 384), v0, f, op_.is_lt, op_.mult)
+
+            def x0hi():
+                ts(c0hi, V("VZ", 128, 256), v0, f, op_.is_lt, op_.mult)
+
+            def x1lo():
+                ts(c1lo, V("VZ", 0, 128), v1, f, op_.is_le, op_.mult)
+                asum(V("S", 1, 2), V("JS"), V("C", 305, 482))
+
+            if t:
+                x0lo()
+                x0hi()
+                asum(V("S", 0, 1), V("J"), V("C", 0, 256))
+                ts(c0ar, V("ZA", 0, K), v0, f, op_.is_lt, op_.mult)
+                ts(c1ar, V("ZA", K, 2 * K), v1, f, op_.is_lt, op_.mult)
+                x1lo()
+            else:
+                x0hi()
+                x1lo()
+                tt(V("VZ", P, 2 * P), V("VZ", 0, P), V("F"), op_.mult)
+                x0lo()
+                asum(V("S", 0, 1), V("J"), V("C", 0, 256))
+            ts(c1hi, V("VZ", 384, 512), v1, f, op_.is_lt, op_.mult)
+            vsum(V("S", 3, 4), V("C", 256, 305))
+            vsum(V("S", 2, 3), c1hi)
+            ts(V("bc", 0, 32), V("zz"), V("S", 0, 1), V("S", 3, 4), op_.add, op_.add)
             ts(V("bc", 32, 64), V("zz"), V("S", 2, 3), V("S", 1, 2), op_.add, op_.add)
             turn(V("RC"), V("bc"))
             for m in range(3):
@@ -281,45 +290,44 @@ def rank_program(g, core, T, topo):
                 qrep(1, 2)
                 mm("b1", P, *rep(1), *own)
                 sact(V("Q1"), V("b1", 0, P), act.Square)
-            ld = "LD%d" % t
             D0, D1, D2, D3 = V("D", 0, 2), V("D", 2, 4), V("D", 4, 6), V("D", 6, 8)
             new = V("PT", W[t], W[t] + K)
-            copy(V(ld, 0, 6, s=2), V("T2", 0, 3))
-            copy(V(ld, 1, 6, s=2), V("T2", 0, 3))
+            gather(new, V("PT", 0, W[t]), lst)
             if more:
                 tt(D0, V("bc", 0, 64, s=32), sl, op_.subtract)
-            gather(V("G6"), V("PT", 0, W[t]), V(ld))
+            if t and more:
+                scatter(V("U"), lp, V("A"))
+            gather(V("G6"), new, V("du"))
             if more:
                 ts(D1, D0, 1.0 / RADIX, float(W[t]), op_.mult, op_.add)
                 ts(D2, D0, float(RADIX * K), None, op_.is_ge)
             turn(V("T6"), V("G6"))
+            if t and more:
+                for t2 in range(t + 1, R):
+                    b = "b%d" % (t2 - t)
+                    mm(b, 128, *rep(t2), *wnd)
+                    sact(V("AQ%d" % t2), V(b, 80, 128), act.Square)
+                scatter(V("Q%d" % (t + 1)), lp, V("AQ%d" % (t + 1)))
             if more:
-                gather(new, V("PT", 0, W[t]), lst)
                 tt(D3, sl, D1, op_.subtract)
             copy(V("LP%d" % t, 0, 3), V("T6", 0, 96, s=32))
-            ts(V("LP%d" % t, 3, 6), V("T6", 0, 96, s=32), float(P), None, op_.add)
-        if t and more:
-            scatter(V("U"), lp, V("A"))
-            for t2 in range(t + 1, R):
-                b = "b%d" % (t2 - t)
-                mm(b, 128, *rep(t2), *wnd)
-                sact(V("AQ%d" % t2), V(b, 80, 128), act.Square)
-            scatter(V("Q%d" % (t + 1)), lp, V("AQ%d" % (t + 1)))
         if more:
-            tt(D3, D3, D2, op_.mult)
-            gather(V("FA"), V("F"), V("LP%d" % t, 0, 3))
             tt(V("U"), V("U"), V("Q%d" % (t + 1)), op_.add)
+            tt(D3, D3, D2, op_.mult)
+            for x in range(2):
+                ts(V("EK", K * x, K * x + K), new, V("pl", x, x + 1), None, op_.is_equal)
+                ts(V("FX", K * x, K * x + K), new, V("pl", x, x + 1), PRED, op_.is_ge, op_.max)
+            scatter(V("U"), V("LP%d" % t, 0, 3), V("big"))
             tt(sl, D1, D3, op_.add)
             ts(V("VZ", 0, P), V("U"), TINY, None, op_.max)
-            ts(V("EK", 0, K), new, V("pl", 0, 1), None, op_.is_equal)
-            ts(V("EK", K, 2 * K), new, V("pl", 1, 2), None, op_.is_equal)
+            if t == 0:
+                quant(V("wc"), V("ws"), V("wb"))
             tt(V("VZ", P, 2 * P), V("VZ", 0, P), V("F"), op_.mult)
             gather(V("OG"), V("VZ", 0, P), V("GL"))
+            for t2 in range(t + 2, R) if t else ():
+                scatter(V("Q%d" % t2), lp, V("AQ%d" % t2))
             turn(V("TC"), V("OG"))
-            for x in range(2):
-                ts(V("EP", 49 * x + K, 49 * x + K + 1), V("TC", 32 * x, 32 * x + 1), V("D", 4 + x, 5 + x), TINY, op_.mult, op_.max)
         if t == 0:
-            quant(V("wc"), V("ws"), V("wb"))
             qrep(2, R)
             for t2 in range(2, R):
                 b = "b%d" % t2
@@ -330,8 +338,6 @@ def rank_program(g, core, T, topo):
                 mm(b, P, *tile(o), *own)
                 sact(V("Y", P * o, P * o + P), V(b, 0, P), act.Copy)
         else:
-            for t2 in range(t + 2, R):
-                scatter(V("Q%d" % t2), lp, V("AQ%d" % t2))
             for o in range(O):
                 b = "b%d" % (6 + o)
                 mm(b, 128, *tile(o), *wnd)
@@ -342,6 +348,9 @@ def rank_program(g, core, T, topo):
                     dma("sa"[o], T.y[:, i:i + P], ap(V("Y", P * o, P * o + P)), [], [V("Y", P * o, P * o + P)])
             if t < R:
                 dma("s", T.y[:, (t - 1) * O * P:t * O * P], ap(V("Y")), [], [V("Y")])
+        if more:
+            for x in range(2):
+                ts(V("EP", 49 * x + K, 49 * x + K + 1), V("TC", 32 * x, 32 * x + 1), V("D", 4 + x, 5 + x), TINY, op_.mult, op_.max)
 
     for q in "vatp":
         wait("p", "s" + q, count[q])

@@ -16,7 +16,7 @@ SCRATCH = {n: ("sbuf", [128, w], d) for n, w, d in (
     ("qc", 128, CODE), ("qs", 128, U8), ("rc", 128 * R, CODE), ("rs", 128 * R, U8), ("wc", 128 * O, CODE), ("ws", 128 * O, U8),
     ("VZ", 2 * P, F32), ("U", P, F32), ("F", P, F32), ("A", K, F32), ("A2", K, F32), ("FX", 2 * K, F32), ("ZA", 2 * K, F32),
     ("EK", 2 * K, F32), ("EP", 2 * K + 2, F32), ("vc", 2, F32), ("pl", 2, F32), ("OG", 64, F32), ("TC", 64, F32), ("big", K, F32),
-    ("C", 2 * (P + K + 1), F32), ("S", 4, F32), ("J", P, F32), ("JS", 177, F32), ("zz", 32, F32), ("bc", 64, F32), ("RC", 64, F32),
+    ("C", 2 * (P + K + 1), F32), ("S", 4, F32), ("J", P, F32), ("JS", P, F32), ("zz", 32, F32), ("bc", 64, F32), ("RC", 64, F32),
     ("E", 195, F32), ("JE", 130, F32), ("Pm", 4, F32), ("T1", 4, F32), ("T2", 4, F32), ("lo", 4, F32), ("hi", 4, F32),
     ("pi", 4, "int32"), ("gi", 4, "int32"), ("pf", 4, F32), ("GL", 4, U16), ("du", 6, U16), ("qo", 8 * R, U16),
     ("PT", P + K * R, F32), ("G6", 96, F32), ("T6", 96, F32), ("D", 8, F32),
@@ -190,6 +190,7 @@ def rank_program(g, core, T, topo):
     ts(V("hi", 0, 3), V("lo", 0, 3), float(RADIX - 1), None, op_.add)
     quant(V("qc"), V("qs"), V("qb"))
     qrep(0, 1)
+    qrep(1, 2)
     own = V("p0c"), V("p0s", 0, P)
     quant(*own, V("cb"))
 
@@ -204,8 +205,17 @@ def rank_program(g, core, T, topo):
     for x in (1, 0):
         ts(V("VZ", 128 * x, 128 * x + 128), V("U", 128 * x, 128 * x + 128), TINY, None, op_.max)
 
+    def gap(k=1):
+        for _ in range(min(k, len(fill_in))):
+            fill_in.pop(0)()
+
+    def store(t):
+        dma("s", T.y[:, t * O * P:(t + 1) * O * P], ap(V("Y")), [], [V("Y")])
+
     for t in range(R + 1):
         more = t + 1 < R
+        fill_in, at_end = [], []
+        D0, D1, D2, D3 = V("D", 0, 2), V("D", 2, 4), V("D", 4, 6), V("D", 6, 8)
         if t:
             n = W[t] if t < R else 128
             log.setdefault("p%dc" % t, []).append((0, 128, n - K, n, True, "net", "arr%d" % (t - 1), NE))
@@ -215,6 +225,44 @@ def rank_program(g, core, T, topo):
             if t < R:
                 mm("b0", 128, *rep(t), *wnd)
                 sact(V("A"), V("b0", 80, 128), act.Square)
+        else:
+            for t2 in range(R):
+                v = V("o%ds" % t2, K, K + PAD)
+                dma("s", ap(v), ap(V("p0s", 0, PAD)), [v], [V("p0s", 0, PAD)])
+        if t < R:
+            n2 = W[t] if more else 80
+            for x in "cs":
+                a, b = V("p%d%s" % (t, x), 0, n2), V("p%d%s" % (t + 1, x), 0, n2)
+                dma("s", u8(b) if x == "c" else ap(b), u8(a) if x == "c" else ap(a), [b], [a])
+            if 1 < t < R - 1:
+                store(t - 2)
+        if t:
+            def later(t2, b):
+                mm(b, 128, *rep(t2), *wnd)
+                sact(V("AQ%d" % t2), V(b, 80, 128), act.Square)
+                fill_in.append(lambda: scatter(V("Q%d" % t2), lp, V("AQ%d" % t2)))
+
+            def result(o):
+                mm("b%d" % (6 + o), 128, *tile(o), *wnd)
+                sact(V("YA", K * o, K * o + K), V("b%d" % (6 + o), 80, 128), act.Copy)
+
+                def put():
+                    scatter(V("Y", P * o, P * o + P), lp, V("YA", K * o, K * o + K))
+                    i = (t - 1) * O * P
+                    if t == R:
+                        dma("sa"[o], T.y[:, i + P * o:i + P * o + P], ap(V("Y", P * o, P * o + P)), [], [V("Y", P * o, P * o + P)])
+                    elif o == O - 1 and t >= R - 2:
+                        store(t - 1)
+                (at_end if t == R - 2 else fill_in).append(put)
+
+            if more:
+                fill_in.append(lambda: scatter(V("U"), lp, V("A")))
+                later(t + 1, "b1")
+            for o in range(O):
+                result(o)
+            for t2 in range(t + 2, R):
+                later(t2, "b%d" % (t2 - t))
+            if t < R:
                 tt(V("EP", 0, K), V("EK", 0, K), V("A"), op_.mult)
                 tt(V("EP", K + 1, 2 * K + 1), V("EK", K, 2 * K), V("A"), op_.mult)
                 ts(V("A2"), V("A"), TINY, None, op_.max)
@@ -222,56 +270,53 @@ def rank_program(g, core, T, topo):
                 vsum(V("vc", 1, 2), V("EP", K + 1, 2 * K + 2), op_.max)
                 for x in range(2):
                     tt(V("ZA", K * x, K * x + K), V("A2"), V("FX", K * x, K * x + K), op_.mult)
+        else:
+            fill_in += [lambda: quant(V("wc"), V("ws"), V("wb")), lambda: qrep(2, 4), lambda: qrep(4, 6)]
         if t < R:
             v0, v1 = V("vc", 0, 1), V("vc", 1, 2)
             f = float(RADIX)
-
-            def x0lo():
-                ts(c0lo, V("VZ", 256, 384), v0, f, op_.is_lt, op_.mult)
-
-            def x0hi():
+            if not t:
                 ts(c0hi, V("VZ", 128, 256), v0, f, op_.is_lt, op_.mult)
-
-            def x1lo():
                 ts(c1lo, V("VZ", 0, 128), v1, f, op_.is_le, op_.mult)
-                asum(V("S", 1, 2), V("JS"), V("C", 305, 482))
-
+                tt(V("VZ", P, 2 * P), V("VZ", 0, P), V("F"), op_.mult)
+            ts(c0lo, V("VZ", 256, 384), v0, f, op_.is_lt, op_.mult)
             if t:
-                x0lo()
-                x0hi()
-                asum(V("S", 0, 1), V("J"), V("C", 0, 256))
+                ts(c0hi, V("VZ", 128, 256), v0, f, op_.is_lt, op_.mult)
+            asum(V("S", 0, 1), V("J"), V("C", 0, 256))
+            if t:
+                ts(c1lo, V("VZ", 0, 128), v1, f, op_.is_le, op_.mult)
+            ts(c1hi, V("VZ", 384, 512), v1, f, op_.is_lt, op_.mult)
+            asum(V("S", 1, 2), V("JS"), V("C", 354, 610))
+            if t:
                 ts(c0ar, V("ZA", 0, K), v0, f, op_.is_lt, op_.mult)
                 ts(c1ar, V("ZA", K, 2 * K), v1, f, op_.is_lt, op_.mult)
-                x1lo()
-            else:
-                x0hi()
-                x1lo()
-                tt(V("VZ", P, 2 * P), V("VZ", 0, P), V("F"), op_.mult)
-                x0lo()
-                asum(V("S", 0, 1), V("J"), V("C", 0, 256))
-            ts(c1hi, V("VZ", 384, 512), v1, f, op_.is_lt, op_.mult)
+                gap(more)
             vsum(V("S", 3, 4), V("C", 256, 305))
-            vsum(V("S", 2, 3), c1hi)
+            vsum(V("S", 2, 3), V("C", 305, 354))
+            gap(not t)
             ts(V("bc", 0, 32), V("zz"), V("S", 0, 1), V("S", 3, 4), op_.add, op_.add)
-            ts(V("bc", 32, 64), V("zz"), V("S", 2, 3), V("S", 1, 2), op_.add, op_.add)
+            ts(V("bc", 32, 64), V("zz"), V("S", 1, 2), V("S", 2, 3), op_.add, op_.add)
             turn(V("RC"), V("bc"))
             for m in range(3):
                 ts(V("E", 65 * m, 65 * m + 64), V("RC"), V("lo", m, m + 1), V("hi", m, m + 1), op_.max, op_.min)
                 if m < 2:
                     asum(V("Pm", m, m + 1), V("JE", 65 * m, 65 * m + 65), V("E", 65 * m, 65 * m + 65))
+            if more:
+                tt(D0, V("bc", 0, 64, s=32), sl, op_.subtract)
             vsum(V("Pm", 2, 3), V("E", 130, 195))
             for a in (0, 64):
                 tt(V("T1", 0, 3, a, a + 64), V("Pm", 0, 3, a, a + 64), V("Pm", 0, 3, 64 - a, 128 - a), op_.add)
+            if more:
+                ts(D1, D0, 1.0 / RADIX, float(W[t]), op_.mult, op_.add)
+                ts(D2, D0, float(RADIX * K), None, op_.is_ge)
             for a in (0, 32, 64, 96):
                 b = a ^ 32
                 tt(V("T2", 0, 3, a, a + 32), V("T1", 0, 3, a, a + 32), V("T1", 0, 3, b, b + 32), op_.add)
+            if more:
+                tt(D3, sl, D1, op_.subtract)
             lst = V("L%d" % t, 0, 3)
             copy(lst, V("T2", 0, 3))
             pick(V("o%dc" % t), V("o%ds" % t, 0, K), V("p%dc" % t), V("p%ds" % t, 0, W[t]), lst)
-            if t == 0:
-                for t2 in range(R):
-                    v = V("o%ds" % t2, K, K + PAD)
-                    dma("s", ap(v), ap(V("p0s", 0, PAD)), [v], [V("p0s", 0, PAD)])
             dst = T.cores[rank ^ PART[t]]
             rid, pid, _e = topo.addr(dst)
             engs = topo.engines(core, dst)[:NE]
@@ -282,53 +327,36 @@ def rank_program(g, core, T, topo):
                 for es, src, out in (
                     (engs[0::2], u8(V("o%dc" % t)), u8(V("p%dc" % (t + 1), n1 - K, n1))),
                     (engs[1::2], ap(V("o%ds" % t)), ap(V("p%ds" % (t + 1), n1 - K, n1 + PAD))))], local_sem=T.sem["sent"])
-            n2 = W[t] if more else 80
-            for x in "cs":
-                a, b = V("p%d%s" % (t, x), 0, n2), V("p%d%s" % (t + 1, x), 0, n2)
-                dma("s", u8(b) if x == "c" else ap(b), u8(a) if x == "c" else ap(a), [b], [a])
-            if t == 0:
-                qrep(1, 2)
-                mm("b1", P, *rep(1), *own)
-                sact(V("Q1"), V("b1", 0, P), act.Square)
-            D0, D1, D2, D3 = V("D", 0, 2), V("D", 2, 4), V("D", 4, 6), V("D", 6, 8)
             new = V("PT", W[t], W[t] + K)
             gather(new, V("PT", 0, W[t]), lst)
-            if more:
-                tt(D0, V("bc", 0, 64, s=32), sl, op_.subtract)
-            if t and more:
-                scatter(V("U"), lp, V("A"))
+            if t == 0:
+                mm("b1", P, *rep(1), *own)
+                sact(V("Q1"), V("b1", 0, P), act.Square)
+            gap(bool(t))
             gather(V("G6"), new, V("du"))
             if more:
-                ts(D1, D0, 1.0 / RADIX, float(W[t]), op_.mult, op_.add)
-                ts(D2, D0, float(RADIX * K), None, op_.is_ge)
+                tt(D3, D3, D2, op_.mult)
+            gap()
             turn(V("T6"), V("G6"))
-            if t and more:
-                for t2 in range(t + 1, R):
-                    b = "b%d" % (t2 - t)
-                    mm(b, 128, *rep(t2), *wnd)
-                    sact(V("AQ%d" % t2), V(b, 80, 128), act.Square)
-                scatter(V("Q%d" % (t + 1)), lp, V("AQ%d" % (t + 1)))
             if more:
-                tt(D3, sl, D1, op_.subtract)
+                tt(V("U"), V("U"), V("Q%d" % (t + 1)), op_.add)
+                tt(sl, D1, D3, op_.add)
             copy(V("LP%d" % t, 0, 3), V("T6", 0, 96, s=32))
         if more:
-            tt(V("U"), V("U"), V("Q%d" % (t + 1)), op_.add)
-            tt(D3, D3, D2, op_.mult)
+            gap()
+            scatter(V("U"), V("LP%d" % t, 0, 3), V("big"))
+            gap()
+            ts(V("VZ", 0, P), V("U"), TINY, None, op_.max)
             for x in range(2):
                 ts(V("EK", K * x, K * x + K), new, V("pl", x, x + 1), None, op_.is_equal)
                 ts(V("FX", K * x, K * x + K), new, V("pl", x, x + 1), PRED, op_.is_ge, op_.max)
-            scatter(V("U"), V("LP%d" % t, 0, 3), V("big"))
-            tt(sl, D1, D3, op_.add)
-            ts(V("VZ", 0, P), V("U"), TINY, None, op_.max)
-            if t == 0:
-                quant(V("wc"), V("ws"), V("wb"))
-            tt(V("VZ", P, 2 * P), V("VZ", 0, P), V("F"), op_.mult)
             gather(V("OG"), V("VZ", 0, P), V("GL"))
-            for t2 in range(t + 2, R) if t else ():
-                scatter(V("Q%d" % t2), lp, V("AQ%d" % t2))
+            tt(V("VZ", P, 2 * P), V("VZ", 0, P), V("F"), op_.mult)
             turn(V("TC"), V("OG"))
+        gap(len(fill_in))
+        for put in at_end:
+            put()
         if t == 0:
-            qrep(2, R)
             for t2 in range(2, R):
                 b = "b%d" % t2
                 mm(b, P, *rep(t2), *own)
@@ -337,17 +365,6 @@ def rank_program(g, core, T, topo):
                 b = "b%d" % (6 + o)
                 mm(b, P, *tile(o), *own)
                 sact(V("Y", P * o, P * o + P), V(b, 0, P), act.Copy)
-        else:
-            for o in range(O):
-                b = "b%d" % (6 + o)
-                mm(b, 128, *tile(o), *wnd)
-                sact(V("YA", K * o, K * o + K), V(b, 80, 128), act.Copy)
-                scatter(V("Y", P * o, P * o + P), lp, V("YA", K * o, K * o + K))
-                if t == R:
-                    i = ((t - 1) * O + o) * P
-                    dma("sa"[o], T.y[:, i:i + P], ap(V("Y", P * o, P * o + P)), [], [V("Y", P * o, P * o + P)])
-            if t < R:
-                dma("s", T.y[:, (t - 1) * O * P:t * O * P], ap(V("Y")), [], [V("Y")])
         if more:
             for x in range(2):
                 ts(V("EP", 49 * x + K, 49 * x + K + 1), V("TC", 32 * x, 32 * x + 1), V("D", 4 + x, 5 + x), TINY, op_.mult, op_.max)

from concourse.bass import DstId, RemoteDMATransfer
from concourse.mybir import dt, AluOpType, AxisListType, ActivationFunctionType

N, P, K, R, O = 8, 256, 48, 6, 2
PART = [1, 2, 4, 1, 2, 4]
NE = 8
W = [P + K * t for t in range(R)]
PRED = 1.0 - 2.0 ** -24
TINY = 2.0 ** -122
PAD = 3 * K
RADIX = 512

F32, CODE, U8, U16, BF = "float32", "float8_e4m3fn_x4", "uint8", "uint16", "bfloat16"
SCRATCH = {n: ("sbuf", [128, w], d) for n, w, d in (
    ("cb", 4 * P, BF), ("qb", 512, BF), ("wb", 512 * O, BF),
    ("qc", 128, CODE), ("qs", 128, U8), ("rc", 128 * R, CODE), ("rs", 128 * R, U8), ("wc", 128 * O, CODE), ("ws", 128 * O, U8),
    ("VZ", 2 * P, F32), ("U", P, F32), ("F", P, F32), ("A", K, F32), ("A2", K, F32), ("FX", 2 * K, F32), ("ZA", 2 * K, F32),
    ("EK", 2 * K, F32), ("EP", 2 * K + 2, F32), ("vc", 2, F32), ("pl", 2, F32), ("OG", 64, F32), ("TC", 64, F32), ("big", K, F32),
    ("C", 2 * (P + K + 1), F32), ("S", 4, F32), ("J", P, F32), ("JS", P, F32), ("zz", 32, F32), ("bc", 64, F32), ("RC", 64, F32),
    ("E", 195, F32), ("JE", 130, F32), ("Pm", 4, F32), ("T1", 4, F32), ("T2", 4, F32), ("lo", 4, F32), ("hi", 4, F32),
    ("pi", 4, "int32"), ("gi", 4, "int32"), ("pf", 4, F32), ("GL", 4, U16), ("du", 6, U16), ("qo", 8 * R, U16),
    ("PT", P + K * R, F32), ("G6", 96, F32), ("T6", 96, F32), ("D", 8, F32),
    ("Y", O * P, F32), ("YA", O * K, F32), ("p6c", 128, CODE), ("p6s", 128 + PAD, U8))}
for _t in range(R):
    for _n, _w, _d in (("p%dc", W[_t], CODE), ("p%ds", W[_t] + PAD, U8), ("o%dc", K, CODE), ("o%ds", K + PAD, U8),
                       ("L%d", 4, U16), ("LP%d", 4, U16), ("Q%d", P, F32), ("AQ%d", K, F32)):
        if _t or _d != F32:
            SCRATCH[_n % _t] = ("sbuf", [128, _w], _d)
for _b in range(8):
    SCRATCH["b%d" % _b] = ("psum", [128, 512], F32)
NDMA = 28
SEMAPHORES = ["sv", "sa", "st", "sp", "sent"] + ["arr%d" % t for t in range(R)] + ["d%d" % i for i in range(NDMA)]


def rank_program(g, core, T, topo):
    rank = T.rank_of(core)
    if rank is None:
        return
    op_ = AluOpType
    act = ActivationFunctionType
    X = AxisListType.X
    queues = {"v": g.vector, "a": g.scalar, "t": g.tensor, "p": g, "s": g.sync}
    count = {"v": 0, "a": 0, "t": 0, "p": 0, "d": 0}
    seen = {}
    log = {}
    psum = {"b%d" % b for b in range(8)}

    def V(n, c0=0, c1=None, p0=0, p1=128, s=1):
        return (n, p0, p1, c0, SCRATCH[n][1][1] if c1 is None else c1, s)

    def ap(v):
        n, p0, p1, c0, c1, s = v
        return T[n][p0:p1, c0:c1] if s == 1 else T[n][p0:p1, c0:c1:s]

    def u8(v):
        return ap(v).bitcast(dt.uint8)

    def wait(q, sem, val):
        if seen.get((q, sem), 0) < val:
            seen[(q, sem)] = val
            queues[q].wait_ge(T.sem[sem], val)

    def order(q, sem, val, writes, reads):
        need = {}
        for views, wr in ((reads, False), (writes, True)):
            for n, p0, p1, c0, c1, s in views:
                whole = n in psum
                for a0, a1, b0, b1, w2, q2, sem2, val2 in log.get(n, ()):
                    if not whole and (a1 <= p0 or p1 <= a0 or b1 <= c0 or c1 <= b0):
                        continue
                    if whole and q2 == q and not (w2 and not wr):
                        continue
                    if not whole and not (w2 or wr):
                        continue
                    if q2 == q and q != "s" and not w2:
                        continue
                    need[sem2] = max(need.get(sem2, 0), val2)
        for s2 in sorted(need):
            wait(q, s2, need[s2])
        for views, wr in ((reads, False), (writes, True)):
            for n, p0, p1, c0, c1, s in views:
                old = log.setdefault(n, [])
                if wr and s == 1:
                    old[:] = [e for e in old if not (p0 <= e[0] and e[1] <= p1 and c0 <= e[2] and e[3] <= c1)]
                old.append((p0, p1, c0, c1, wr, q, sem, val))

    def op(q, writes, reads, fn):
        count[q] += 1
        sem = "s" + q
        order(q, sem, count[q], writes, reads)
        fn().then_inc(T.sem[sem], 1)

    def dma(q, out, in_, writes, reads):
        sem = "d%d" % count["d"]
        count["d"] += 1
        order(q, sem, 16, writes, reads)
        queues[q].dma_start(out, in_).then_inc(T.sem[sem], 16)

    def ts(out, in0, s1, s2, o0, o1=None):
        r = [in0] + [s for s in (s1, s2) if isinstance(s, tuple)]
        a1 = ap(s1) if isinstance(s1, tuple) else s1
        a2 = ap(s2) if isinstance(s2, tuple) else s2
        if o1 is None:
            op("v", [out], r, lambda: g.vector.tensor_scalar(ap(out), ap(in0), a1, None, o0))
        else:
            op("v", [out], r, lambda: g.vector.tensor_scalar(ap(out), ap(in0), a1, a2, o0, o1))

    def tt(out, a, b, o):
        op("v", [out], [a, b], lambda: g.vector.tensor_tensor(ap(out), ap(a), ap(b), o))

    def copy(out, a):
        op("v", [out], [a], lambda: g.vector.tensor_copy(ap(out), ap(a)))

    def gather(out, win, off):
        op("v", [out], [win, off], lambda: g.vector.tensor_copy(ap(out), ap(win).indirect(ap(off))))

    def scatter(win, off, a):
        op("v", [win], [a, off], lambda: g.vector.tensor_copy(ap(win).indirect(ap(off)), ap(a)))

    def turn(out, a):
        op("v", [out], [a], lambda: g.vector.transpose(ap(out), ap(a)))

    def fill(v, x):
        op("v", [v], [], lambda: g.vector.memset(ap(v), x))

    def sact(out, a, f):
        op("a", [out], [a], lambda: g.scalar.activation(ap(out), ap(a), f))

    def asum(out, junk, a):
        op("a", [out, junk], [a], lambda: g.scalar.activation(ap(junk), ap(a), act.Copy, accum_out=ap(out)))

    def vsum(out, a, o=op_.add):
        op("v", [out], [a], lambda: g.vector.tensor_reduce(ap(out), ap(a), X, o))

    def quant(c, s, a):
        op("v", [c, s], [a], lambda: g.vector.quantize_mx(ap(c), ap(s), ap(a)))

    def mm(bank, n, lc, ls, rc, rs):
        out = V(bank, 0, n)
        op("t", [out], [lc, ls, rc, rs], lambda: g.tensor.matmul_mx(ap(out), ap(lc), ap(ls), ap(rc), ap(rs), True, True))

    def pick(oc, os, c, s, off):
        op("v", [oc], [c, off], lambda: g.vector.tensor_copy(ap(oc).bitcast(dt.uint32), ap(c).bitcast(dt.uint32).indirect(ap(off))))
        op("a", [os], [s, off], lambda: g.scalar.activation(ap(os), ap(s).indirect(ap(off)), act.Copy))

    def qrep(a, b):
        pick(V("rc", 128 * a, 128 * b), V("rs", 128 * a, 128 * b), V("qc"), V("qs"), V("qo", 8 * a, 8 * b))

    def rep(t):
        return V("rc", 128 * t, 128 * t + 128), V("rs", 128 * t, 128 * t + 128)

    def tile(o):
        return V("wc", 128 * o, 128 * o + 128), V("ws", 128 * o, 128 * o + 128)

    def whole(v, out, **k):
        op("p", [v], [], lambda: g.iota(ap(v), *out, **k))

    dma("s", ap(V("cb")), T.c[:], [V("cb")], [])
    dma("a", ap(V("qb")), T.qt[:], [V("qb")], [])
    dma("s", ap(V("wb")), T.w[:], [V("wb")], [])
    c0lo, c0hi, c0ar = V("C", 0, 128), V("C", 128, 256), V("C", 256, 304)
    sl = V("C", 304, 306)
    c1ar, c1lo, c1hi = V("C", 306, 354), V("C", 354, 482), V("C", 482, 610)
    fl = {"allow_small_or_imprecise_dtypes": True}
    whole(V("pi", 0, 1), ([[0, 1]], 0, 1))
    whole(V("gi"), ([[128, 2], [16, 2]], 0, 0))
    whole(sl, ([[128, 2]], 0, 1), **fl)
    whole(V("pl"), ([[128, 2]], 0, 1), **fl)
    whole(V("PT", 0, P), ([[1, P]], 0, 0), **fl)
    fill(V("F"), PRED)
    op("p", [V("F")], [V("F")], lambda: g.affine_select(ap(V("F")), ap(V("F")), [[0, 2], [-1, 128]], op_.is_gt, 1.0, 0, 1))
    for t in range(R):
        fill(V("qo", 8 * t, 8 * t + 8), t)
    fill(V("zz"), 0.0)
    fill(V("E"), 0.0)
    fill(c0ar, 0.0)
    fill(c1ar, 0.0)
    fill(V("big"), 1e29)
    ts(V("pi", 1, 2), V("pi", 0, 1), 0x6F, None, op_.bitwise_and)
    ts(V("pi", 2, 3), V("pi", 0, 1), 0x0F, None, op_.bitwise_and)
    copy(V("pf", 1, 3), V("pi", 1, 3))
    ts(V("GL"), V("gi"), V("pf", 1, 2), None, op_.add)
    ts(V("big"), V("big"), 1e9, None, op_.mult)
    span = P * RADIX - (RADIX - 1)
    for m in range(3):
        ts(V("lo", m, m + 1), V("pf", 2, 3), float(RADIX), float(16 * RADIX * m), op_.mult, op_.add)
        ts(V("E", 65 * m + 64, 65 * m + 65, 0, 32), V("pf", 2, 3, 0, 32), float(-span), float(-(span * 16 * m + (RADIX - 1) * (P - 1))), op_.mult, op_.add)
        for j in (2 * m, 2 * m + 1):
            ts(V("du", j, j + 1), V("pf", 2, 3), float(16 * m), None, op_.add)
    ts(V("hi", 0, 3), V("lo", 0, 3), float(RADIX - 1), None, op_.add)
    quant(V("qc"), V("qs"), V("qb"))
    qrep(0, 1)
    qrep(1, 2)
    own = V("p0c"), V("p0s", 0, P)
    quant(*own, V("cb"))

    mm("b0", P, *rep(0), *own)
    for x in range(2):
        mm("b%d" % (6 + x), 128, V("p0c", 128 * x, 128 * x + 128), V("p0s", 128 * x, 128 * x + 128), V("qc"), V("qs"))
    for x in (1, 0):
        sact(V("U", 128 * x, 128 * x + 128), V("b0", 128 * x, 128 * x + 128), act.Square)
    for x in range(2):
        s0 = V("b%d" % (6 + x), 0, 1)
        ts(V("vc", x, x + 1), s0, s0, TINY, op_.mult, op_.max)
    for x in (1, 0):
        ts(V("VZ", 128 * x, 128 * x + 128), V("U", 128 * x, 128 * x + 128), TINY, None, op_.max)

    def gap(k=1):
        for _ in range(min(k, len(fill_in))):
            fill_in.pop(0)()

    def store(t):
        dma("s", T.y[:, t * O * P:(t + 1) * O * P], ap(V("Y")), [], [V("Y")])

    for t in range(R + 1):
        more = t + 1 < R
        fill_in, at_end = [], []
        D0, D1, D2, D3 = V("D", 0, 2), V("D", 2, 4), V("D", 4, 6), V("D", 6, 8)
        if t:
            n = W[t] if t < R else 128
            log.setdefault("p%dc" % t, []).append((0, 128, n - K, n, True, "net", "arr%d" % (t - 1), NE))
            log.setdefault("p%ds" % t, []).append((0, 128, n - K, n + PAD, True, "net", "arr%d" % (t - 1), NE))
            wnd = V("p%dc" % t, n - 128, n), V("p%ds" % t, n - 128, n)
            lp = V("LP%d" % (t - 1), 0, 3)
            if t < R:
                mm("b0", 128, *rep(t), *wnd)
                sact(V("A"), V("b0", 80, 128), act.Square)
        else:
            for t2 in range(R):
                v = V("o%ds" % t2, K, K + PAD)
                dma("s", ap(v), ap(V("p0s", 0, PAD)), [v], [V("p0s", 0, PAD)])
        if t < R:
            n2 = W[t] if more else 80
            for x in "cs":
                a, b = V("p%d%s" % (t, x), 0, n2), V("p%d%s" % (t + 1, x), 0, n2)
                dma("s", u8(b) if x == "c" else ap(b), u8(a) if x == "c" else ap(a), [b], [a])
            if 1 < t < R - 1:
                store(t - 2)
        if t:
            def later(t2, b):
                mm(b, 128, *rep(t2), *wnd)
                sact(V("AQ%d" % t2), V(b, 80, 128), act.Square)
                fill_in.append(lambda: scatter(V("Q%d" % t2), lp, V("AQ%d" % t2)))

            def result(o):
                mm("b%d" % (6 + o), 128, *tile(o), *wnd)
                sact(V("YA", K * o, K * o + K), V("b%d" % (6 + o), 80, 128), act.Copy)

                def put():
                    scatter(V("Y", P * o, P * o + P), lp, V("YA", K * o, K * o + K))
                    i = (t - 1) * O * P
                    if t == R:
                        dma("sa"[o], T.y[:, i + P * o:i + P * o + P], ap(V("Y", P * o, P * o + P)), [], [V("Y", P * o, P * o + P)])
                    elif o == O - 1 and t >= R - 2:
                        store(t - 1)
                (at_end if t == R - 2 else fill_in).append(put)

            if more:
                fill_in.append(lambda: scatter(V("U"), lp, V("A")))
                later(t + 1, "b1")
            for o in range(O):
                result(o)
            for t2 in range(t + 2, R):
                later(t2, "b%d" % (t2 - t))
            if t < R:
                tt(V("EP", 0, K), V("EK", 0, K), V("A"), op_.mult)
                tt(V("EP", K + 1, 2 * K + 1), V("EK", K, 2 * K), V("A"), op_.mult)
                ts(V("A2"), V("A"), TINY, None, op_.max)
                vsum(V("vc", 0, 1), V("EP", 0, K + 1), op_.max)
                vsum(V("vc", 1, 2), V("EP", K + 1, 2 * K + 2), op_.max)
                for x in range(2):
                    tt(V("ZA", K * x, K * x + K), V("A2"), V("FX", K * x, K * x + K), op_.mult)
        else:
            fill_in += [lambda: quant(V("wc"), V("ws"), V("wb")), lambda: qrep(2, 4), lambda: qrep(4, 6)]
        if t < R:
            v0, v1 = V("vc", 0, 1), V("vc", 1, 2)
            f = float(RADIX)
            if not t:
                ts(c0hi, V("VZ", 128, 256), v0, f, op_.is_lt, op_.mult)
                ts(c1lo, V("VZ", 0, 128), v1, f, op_.is_le, op_.mult)
                tt(V("VZ", P, 2 * P), V("VZ", 0, P), V("F"), op_.mult)
            ts(c0lo, V("VZ", 256, 384), v0, f, op_.is_lt, op_.mult)
            if t:
                ts(c0hi, V("VZ", 128, 256), v0, f, op_.is_lt, op_.mult)
            asum(V("S", 0, 1), V("J"), V("C", 0, 256))
            if t:
                ts(c1lo, V("VZ", 0, 128), v1, f, op_.is_le, op_.mult)
            ts(c1hi, V("VZ", 384, 512), v1, f, op_.is_lt, op_.mult)
            asum(V("S", 1, 2), V("JS"), V("C", 354, 610))
            if t:
                ts(c0ar, V("ZA", 0, K), v0, f, op_.is_lt, op_.mult)
                ts(c1ar, V("ZA", K, 2 * K), v1, f, op_.is_lt, op_.mult)
                gap(more)
            vsum(V("S", 3, 4), V("C", 256, 305))
            vsum(V("S", 2, 3), V("C", 305, 354))
            gap(not t)
            ts(V("bc", 0, 32), V("zz"), V("S", 0, 1), V("S", 3, 4), op_.add, op_.add)
            ts(V("bc", 32, 64), V("zz"), V("S", 1, 2), V("S", 2, 3), op_.add, op_.add)
            turn(V("RC"), V("bc"))
            for m in range(3):
                ts(V("E", 65 * m, 65 * m + 64), V("RC"), V("lo", m, m + 1), V("hi", m, m + 1), op_.max, op_.min)
                if m < 2:
                    asum(V("Pm", m, m + 1), V("JE", 65 * m, 65 * m + 65), V("E", 65 * m, 65 * m + 65))
            if more:
                tt(D0, V("bc", 0, 64, s=32), sl, op_.subtract)
            vsum(V("Pm", 2, 3), V("E", 130, 195))
            for a in (0, 64):
                tt(V("T1", 0, 3, a, a + 64), V("Pm", 0, 3, a, a + 64), V("Pm", 0, 3, 64 - a, 128 - a), op_.add)
            if more:
                ts(D1, D0, 1.0 / RADIX, float(W[t]), op_.mult, op_.add)
                ts(D2, D0, float(RADIX * K), None, op_.is_ge)
            for a in (0, 32, 64, 96):
                b = a ^ 32
                tt(V("T2", 0, 3, a, a + 32), V("T1", 0, 3, a, a + 32), V("T1", 0, 3, b, b + 32), op_.add)
            if more:
                tt(D3, sl, D1, op_.subtract)
            lst = V("L%d" % t, 0, 3)
            copy(lst, V("T2", 0, 3))
            pick(V("o%dc" % t), V("o%ds" % t, 0, K), V("p%dc" % t), V("p%ds" % t, 0, W[t]), lst)
            dst = T.cores[rank ^ PART[t]]
            rid, pid, _e = topo.addr(dst)
            engs = topo.engines(core, dst)[:NE]
            n1 = W[t + 1] if more else 128
            order("p", "sent", 0, [], [V("o%dc" % t), V("o%ds" % t)])
            g.remote_dma_fused([
                RemoteDMATransfer(dst_ids=[DstId(rid=rid, pnc=pid)], dma_engine_mask=sum(1 << e for e in es), remote_sem=T.sem["arr%d" % t], src=src, dst=out)
                for es, src, out in (
                    (engs[0::2], u8(V("o%dc" % t)), u8(V("p%dc" % (t + 1), n1 - K, n1))),
                    (engs[1::2], ap(V("o%ds" % t)), ap(V("p%ds" % (t + 1), n1 - K, n1 + PAD))))], local_sem=T.sem["sent"])
            new = V("PT", W[t], W[t] + K)
            gather(new, V("PT", 0, W[t]), lst)
            if t == 0:
                mm("b1", P, *rep(1), *own)
                sact(V("Q1"), V("b1", 0, P), act.Square)
            gap(bool(t))
            gather(V("G6"), new, V("du"))
            if more:
                tt(D3, D3, D2, op_.mult)
            gap()
            turn(V("T6"), V("G6"))
            if more:
                tt(V("U"), V("U"), V("Q%d" % (t + 1)), op_.add)
                tt(sl, D1, D3, op_.add)
            copy(V("LP%d" % t, 0, 3), V("T6", 0, 96, s=32))
        if more:
            gap()
            scatter(V("U"), V("LP%d" % t, 0, 3), V("big"))
            gap()
            ts(V("VZ", 0, P), V("U"), TINY, None, op_.max)
            for x in range(2):
                ts(V("EK", K * x, K * x + K), new, V("pl", x, x + 1), None, op_.is_equal)
                ts(V("FX", K * x, K * x + K), new, V("pl", x, x + 1), PRED, op_.is_ge, op_.max)
            gather(V("OG"), V("VZ", 0, P), V("GL"))
            tt(V("VZ", P, 2 * P), V("VZ", 0, P), V("F"), op_.mult)
            turn(V("TC"), V("OG"))
        gap(len(fill_in))
        for put in at_end:
            put()
        if t == 0:
            for t2 in range(2, R):
                b = "b%d" % t2
                mm(b, P, *rep(t2), *own)
                sact(V("Q%d" % t2), V(b, 0, P), act.Square)
            for o in range(O):
                b = "b%d" % (6 + o)
                mm(b, P, *tile(o), *own)
                sact(V("Y", P * o, P * o + P), V(b, 0, P), act.Copy)
        if more:
            for x in range(2):
                ts(V("EP", 49 * x + K, 49 * x + K + 1), V("TC", 32 * x, 32 * x + 1), V("D", 4 + x, 5 + x), TINY, op_.mult, op_.max)

    for q in "vatp":
        wait("p", "s" + q, count[q])
    for i in range(count["d"]):
        wait("p", "d%d" % i, 16)
    for t in range(R):
        wait("p", "arr%d" % t, NE)
    wait("p", "sent", NE * R)
